import numpy as np, ml_dtypes
CORES = [24,25,26,27,28,29,30,31]
N = 8
import mx_ref
BF = ml_dtypes.bfloat16
def gcols(t, e):
    v = np.concatenate([t.reshape(8, 16, -1, 4), np.zeros((8, 16, 1, 4), BF)], axis=2)
    return np.ascontiguousarray(np.stack([v[g][:, e[g]] for g in range(8)])).reshape(128, -1)
def tile(rs):
    return np.stack(rs, axis=2).reshape(128, -1).astype(BF)
def pick(q, e):
    c = np.concatenate([q[0].reshape(128, -1, 4), np.zeros((128, 1, 4), np.uint8)], axis=1); s = np.concatenate([q[1], np.ones((16, 1), np.uint8)], axis=1)
    return (np.ascontiguousarray(c[:, e].reshape(128, -1)), np.ascontiguousarray(s[:, e]))
def join(*qs):
    return (np.concatenate([q[0] for q in qs], axis=1), np.concatenate([q[1] for q in qs], axis=1))
def put(q, e, v):
    c, s = q[0].reshape(128, -1, 4).copy(), q[1].copy(); c[:, e] = v[0].reshape(128, -1, 4); s[:, e] = v[1]
    return (c.reshape(128, -1), s)
def pk(c, s):
    return (np.ascontiguousarray(c), mx_ref.live(s))
def emit(q):
    return q[0], q[1]
def packed(v, rng):
    q = [mx_ref.quantize(np.ascontiguousarray(v[r])) for r in range(N)]
    return np.stack([a for a, b in q]), np.stack([mx_ref.plane(b, rng) for a, b in q])
def values_of_codes():
    e, c = np.zeros((128, 128, 4), np.float32), np.zeros((128, 2, 4), np.uint8)
    e[np.arange(128), np.arange(128), 0] = 1
    c[:127, :, 0] = np.arange(256).reshape(2, 128).T[:127]
    return mx_ref.matmul(mx_ref.quantize(e.reshape(128, 512).astype(BF)), (c.reshape(128, 8), np.full((16, 2), 127, np.uint8))).T.reshape(-1).astype(np.float64)
CODE_VALUE, SCALE_VALUE = values_of_codes(), 2.0 ** (np.arange(256) - 127.0)
def decode(q):
    return (CODE_VALUE[q[0]].reshape(16, 8, -1, 4) * SCALE_VALUE[q[1]][:, None, :, None] + 0.0).reshape(128, -1).astype(np.float32)
def f(rng, *shape):
    return mx_ref.flush((rng.standard_normal(shape, dtype=np.float32) * np.exp2(rng.integers(-2, 3, shape[:-1] + (1,)))).astype(BF))
def wide(rng, *shape, cols=0):
    v = rng.standard_normal(shape, dtype=np.float32) * np.exp2(rng.integers(-12, 13, shape)).astype(np.float32)
    if cols: v *= np.repeat(np.exp2(rng.integers(-cols, cols + 1, shape[:-2] + (1, shape[-1] // 4))) * (rng.random(shape[:-2] + (1, shape[-1] // 4)) > 0.0625), 4, axis=-1).astype(np.float32)
    return mx_ref.flush(v.astype(BF))
C, R = 320, 2
def alike(w):
    return np.stack([w] * N)
def layers(rng):
    return f(rng, N, 128, 4096)
def weights(rng, w, still=()):
    w = np.array(w).reshape(N, 8, 16, 8, 8, 16, 4)
    for i in still:
        w[:, :, i] = 0
        w[:, :, :, :, :, i] = 0
    c, p = packed(w.reshape(N, 128, 4096), rng)
    return {"wc": c, "ws": p}
def numbers_of(rng):
    return {"x": np.array(f(rng, N, 128, 4 * C)), "u": alike(f(rng, 128, 512)), "v": np.array(f(rng, N, 128, 512))}
def unscored(rng):
    a = np.array(f(rng, 128, 512)).reshape(128, 128, 4)
    a[:, ::16] = 0
    a[:, 1::16] = 0
    return a
def setup_inputs(rng):
    return {**numbers_of(rng), **weights(rng, layers(rng))}
def setup_inputs_ties(rng):
    d = numbers_of(rng)
    o = rng.permutation(N)
    k = rng.integers(0, 3, (N, 8, C))
    m = np.where((o % 2 == 0)[:, None, None], k, rng.integers(-2, 3, (N, 8, C)))
    k[o == 0] = 0
    m[o == 0] = 0
    k[o == 1] *= -1
    x = d["x"].reshape(N, 8, 16, C, 4)
    x[:, :, 0] = 0
    x[:, :, 0, :, 0] = k.astype(np.float32).astype(BF)
    x[:, :, 0, :, 1] = m.astype(np.float32).astype(BF)
    a = unscored(rng)
    for h in range(0, 128, 16):
        a[h, h, 0] = 1
        a[h, h + 1, 1] = 1
    return {"x": x.reshape(N, 128, 4 * C), "u": alike(a.reshape(128, 512)), "v": d["v"], **weights(rng, layers(rng), [0])}
def setup_inputs_near(rng):
    d = numbers_of(rng)
    x = d["x"].astype(np.float32).reshape(N, 8, 16, C, 4)
    x[:, :, 0] = 0
    x[:, :, 8:] = 0
    a = unscored(rng)
    o = rng.permutation(8) % 4
    for g in range(8):
        h = 16 * g
        for m in range(2):
            s = rng.integers(0, 16, (N, C))
            c = rng.integers(0, 2, (N, C)) * 2.0 - 1.0
            if o[g] < 3: x[:, g, 8 + m] = ((s[:, :, None] >> np.arange(4)) & 1) * np.exp2(np.arange(4) - 23.0)
            if o[g] < 2:
                k = 1.0 if o[g] == 0 else 2.0 ** -30
                x[:, g, 0, :, m] = c
                x[:, g, 11, :, 0] = 2.0 ** -10
                a[h, h + m, m] = k
                a[h + 8 + m, h + m] = k
                a[h + 11, h + m, 0] = k
            elif o[g] == 2:
                for r in range(N): x[r, g, 0, rng.permutation(C)[:2], m] = [1.0, -1.0]
                a[h, h + m, m] = 2.0 ** 30
                a[h + 8 + m, h + m] = 2.0 ** -30
            else:
                x[:, g, 10, :, m] = np.where(s % 2 == 0, 1.125 * 2.0 ** -30 * c, 0.0)
                x[:, g, 12, :, m] = np.where(s % 2 == 0, 0.0, 1.25 * 2.0 ** -30 * c)
                a[h + 10, h + m, m] = 1.125 * 2.0 ** -30
                a[h + 12, h + m, m] = 2.0 ** -30
    return {"x": x.reshape(N, 128, 4 * C).astype(BF), "u": alike(a.reshape(128, 512)), "v": d["v"], **weights(rng, layers(rng), [0, 8, 9, 10, 11, 12, 13, 14, 15])}
def setup_inputs_odd(rng):
    d = numbers_of(rng)
    a = (1.0 + (2 * rng.integers(0, 64, (N, 16, 8, C, 4)) + 1) * 2.0 ** -7) * np.exp2(-rng.integers(8, 15, (N, 16, 8, C, 4)).astype(np.float64))
    a = np.where(np.arange(8)[:, None, None] * 4 + np.arange(4) == rng.integers(0, 32, (N, 16, 1, C, 1)), 1.96875, a)
    a = a * (rng.integers(0, 2, a.shape) * 2.0 - 1.0) * np.exp2(rng.integers(-2, 3, (N, 16, 1, C, 1)).astype(np.float64))
    return {"x": a.astype(np.float32).reshape(N, 128, 4 * C).astype(BF), "u": d["u"], "v": d["v"], **weights(rng, layers(rng), [8, 9, 10, 11, 12, 13, 14, 15])}
def setup_inputs_ends(rng):
    d = numbers_of(rng)
    o = rng.permutation(N) % 4
    x = np.zeros((N, 8, 16, C, 4), np.float32)
    x[:, :, 8:12] = f(rng, N, 8, 4, C, 4).astype(np.float32) * np.float32(1024)
    for r in range(N):
        c = rng.integers(0, 2, C) * 2.0 - 1.0
        w = rng.choice([1.375, 1.5], (8, C))
        a, b = rng.permutation(C)[:2]
        w[:, b] = 1.625
        if o[r] == 0:
            w[:, a] = 1.625
            c[a], c[b] = 1.0, -1.0
        else: w[:, a] = 1.25
        if o[r] == 1: c[:] = -1.0
        if o[r] == 2: c[:] = 1.0
        e = w * c * 2.0 ** 29 if o[r] < 2 else np.ones((8, 1)) * c * 2.0 ** -30
        x[r, :, :8] = e[:, None, :, None]
        k = (rng.integers(0, 2, (128, 512)) * 2.0 - 1.0).astype(np.float32)
        if o[r] == 1: d["v"][r] = (k * np.float32(2.0 ** 30)).astype(BF)
        if o[r] == 2: d["v"][r] = (k * np.float32(2.0 ** -30)).astype(BF)
    u = unscored(rng).reshape(8, 16, 128, 4)
    p = rng.permutation(8)
    for g in range(8):
        k = (2.0 ** 30 if p[g] < 4 else 2.0 ** -29) * (1.0 if p[g] % 2 == 0 else -1.0)
        for m in range(2):
            u[:, :8, 16 * g + m] = 0.75 * k * (1 - 2 * m)
            u[g, :8, 16 * g + m] = k * (1 - 2 * m)
    w = ((rng.integers(0, 2, (N, 128, 4096)) * 2.0 - 1.0) * 2.0 ** -11).astype(np.float32).astype(BF)
    return {"x": x.reshape(N, 128, 4 * C).astype(BF), "u": alike(u.reshape(128, 512)), "v": d["v"], **weights(rng, w, [0, 1, 2, 3, 4, 5, 6, 7])}
def setup_inputs_spread(rng):
    d = numbers_of(rng)
    w = np.array(mx_ref.flush((layers(rng).astype(np.float32) * np.float32(2.0 ** -7)).astype(BF)))
    x = np.array(wide(rng, N, 128, 4 * C, cols=3))
    e = int(rng.integers(N))
    x[e] = ((1.0 + 0.25 * rng.random((128, 4 * C))) * 2.0 ** 24).astype(np.float32).astype(BF)
    w[e ^ 1] = (-0.1875 - 0.0625 * rng.random((128, 4096))).astype(np.float32).astype(BF)
    return {"x": x, "u": d["u"], "v": d["v"], **weights(rng, w)}
def check_inputs(d):
    b = []
    for k in ("x", "u", "v"):
        a = np.abs(d[k].astype(np.float32))
        if not (np.isfinite(a).all() and ((a == 0) | (a >= 2.0 ** -30) & (a <= 2.0 ** 30)).all()): b.append("a value of " + k)
    if (d["u"] != d["u"][:1]).any(): b.append("u isn't the same on all ranks")
    none, least, most = [emit(mx_ref.quantize(np.full((128, 16), k, np.float32).astype(BF)))[1][0, 0] for k in (0.0, 2.0 ** -30, 2.0 ** 30)]
    size = 0.0
    for r in range(N):
        if ((d["wc"][r] == 0x7F) | (d["wc"][r] == 0xFF)).any(): b.append("wc: a code that is no number")
        s = mx_ref.live(d["ws"][r])
        if ((s != none) & ((s < least) | (s > most))).any(): b.append("ws: a scale out of range")
        if (((d["wc"][r].reshape(16, 8, -1, 4) & 0x7F) != 0) & (s == none)[:, None, :, None]).any(): b.append("wc: a code other than zero where the scale is that of zeros")
        size = max(size, float(np.abs(decode(pk(d["wc"][r], d["ws"][r]))).max()))
    if not float(np.abs(d["x"].astype(np.float32)).max()) * (1.0 + 20.0 * size) * (1.0 + 20.0 * size) <= 900000000.0: b.append("the sizes of x and W together")
    return b
def places(s):
    o = np.argsort(-s, axis=1, kind="stable")
    i = np.zeros(s.shape, np.int64)
    np.put_along_axis(i, o, np.broadcast_to(np.arange(C), s.shape), axis=1)
    return o, i
def reference(x, u, v, wc, ws):
    qu = [mx_ref.quantize(u[r]) for r in range(N)]
    lay = [pk(wc[r], ws[r]) for r in range(N)]
    now = [x[r] for r in range(N)]
    total = np.zeros((N, C), np.int64)
    for t in range(R):
        q = [mx_ref.quantize(now[r]) for r in range(N)]
        full = [decode(q[r]).astype(BF) for r in range(N)]
        s = [mx_ref.matmul(qu[r], q[r]) + np.float32(0.0) for r in range(N)]
        first = [places(s[r][::16]) for r in range(N)]
        second = [places(s[r][1::16])[1] for r in range(N)]
        made = [None] * N
        for r in range(N):
            e = r ^ (1 << t)
            total[r] = first[r][1][0]
            took = np.zeros((8, C), np.int64)
            for g in range(8):
                turn = places(total[r][None])[1][0]
                took[g] = first[e][0][g][turn]
                total[r] = total[r] + second[e][g][took[g]]
            z = mx_ref.quantize(gcols(full[e], took))
            p = [mx_ref.matmul(pick(lay[r], np.arange(128 * b, 128 * b + 128)), z) for b in range(8)]
            y = tile([np.maximum(p[b], p[b + 4]) * np.float32(0.03125) for b in range(4)])
            back = gcols(decode(mx_ref.quantize(y)).astype(BF), np.argsort(took, axis=1))
            made[e] = (full[e].astype(np.float32) + back.astype(np.float32)).astype(BF)
        now = made
    y, tot = np.zeros((N, 128, C), np.float32), np.zeros((N, 1, C), np.float32)
    oc, osc = np.zeros((N, 128, 4 * C), np.uint8), np.zeros((N, 16, C), np.uint8)
    for r in range(N):
        q = mx_ref.quantize(now[r])
        y[r] = mx_ref.matmul(mx_ref.quantize(v[r]), q)
        tot[r, 0] = total[r]
        oc[r], osc[r] = emit(q)
    return {"y": y, "tot": tot, "oc": oc, "osc": osc}

@@ -1,0 +1,447 @@
+from concourse.mybir import dt, AluOpType as A, AxisListType, ActivationFunctionType as F
+
+NC = 320
+NP = 384
+NG = 8
+NM = 20
+RING = 6
+
+F32, BF, I32, U16, FP8, U8 = "float32", "bfloat16", "int32", "uint16", "float8_e4m3fn_x4", "uint8"
+SCRATCH = {"ps": ("psum", [128, 4096], F32)}
+
+
+def _sb(name, cols, dtype):
+    SCRATCH[name] = ("sbuf", [128, cols], dtype)
+
+
+def _mx(name, cols):
+    _sb(name + "c", cols, FP8)
+    _sb(name + "s", cols, U8)
+
+
+for _n, _c in (("ipr", NC), ("diag", NC), ("rst", NC), ("tab0", NC), ("tier", NC), ("iot", NC), ("hcol", 1), ("pif", 1),
+               ("mask8", 8), ("mask8n", 8), ("h8", 8), ("tiec", 4), ("bdi", 512), ("triv", 128), ("lf", 48), ("far", 1),
+               ("a0", 4), ("d0", 4), ("dA", NC), ("dB", NC), ("scA", NC), ("scB", NC), ("sxA", NC), ("sxB", NC),
+               ("accA", NM), ("accB", NM), ("eeA", NC), ("eeB", NC), ("plA", NM), ("plB", NM),
+               ("bxe", NC), ("bx", NC), ("cx", NC), ("ir", NC), ("di", NC), ("si", NC),
+               ("xn", 24), ("kr0", NC), ("kr1", NC), ("pk", 4), ("cnt", 4), ("og", 48), ("ogd", 48), ("os1", 48),
+               ("sr", NC), ("rk", NC), ("rkd", NC), ("rks", NC), ("cc0", NC), ("cc1", NC), ("ysb", NC), ("tsb", NC), ("cw", NG * NC)):
+    _sb(_n, _c, F32)
+for _n, _c in (("xt0", 4 * NP), ("xt1", 4 * NP), ("ut", 512), ("vt", 512), ("ones", 512), ("ident", 128), ("et", 2048), ("wg", 4096),
+               ("bd", 512), ("bg", 960), ("tri", NC), ("tri128", 128), ("a0c", 3 * 448), ("eqb", 128), ("eq", NC), ("tq", NC),
+               ("junk", 4 * 448), ("cb", 328), ("ct", 4 * NC), ("nt", 512), ("zt", 4 * NC), ("yt", 4 * NC),
+               ("cmp", RING * NC), ("fp", 4 * NC), ("fs", 4 * NC), ("yp", 4 * NC)):
+    _sb(_n, _c, BF)
+_sb("pi_i", 4, I32)
+for _n, _c in (("l15", NM), ("lm", NM), ("lu", 24), ("aoff", NM), ("inva", NM), ("off", NM), ("offo", 4), ("noff", NM), ("koff", NM)):
+    _sb(_n, _c, U16)
+KE, KW, KB, KG = 0, 512, 1536, 1664
+for _n, _c in (("xq0", NP), ("xq1", NP), ("xq2", NC), ("px0", NC), ("px1", NC), ("py0", NC), ("py1", NC), ("uq", 128), ("up", 384), ("vq", 128),
+               ("kq", 1904), ("nq", 128), ("cq", NC), ("zq", NC), ("yq0", NC), ("yq1", NC), ("ww", 1024)):
+    _mx(_n, _c)
+
+SEMAPHORES = ["v", "s", "t", "gp", "ls"] + ["d%d" % k for k in range(16)] + ["rx%d" % k for k in range(8)]
+
+MG16 = 1.5 * 2.0 ** 27
+MG32 = 1.5 * 2.0 ** 28
+
+
+def rank_program(g, core, T, topo):
+    rank = T.rank_of(core)
+    if rank is None:
+        return
+    V, S, PE = g.vector, g.scalar, g.tensor
+    queues = {"v": V, "s": S, "t": PE, "gp": g, "sy": g.sync}
+    known = {q: {} for q in queues}
+    count = {"v": 0, "s": 0, "t": 0, "gp": 0}
+    state = {}
+    tally = {"dma": 0, "ls": 0, "ring": 0, "junk": 0}
+
+    def st(k):
+        if k not in state:
+            state[k] = {"w": [], "r": [], "b": []}
+        return state[k]
+
+    def waits(eng, r, w, p):
+        deps = []
+        for k in r:
+            x = st(k)
+            deps += x["w"] + x["b"]
+            if k[:2] == "ps":
+                deps += [d for d in x["r"] if d[0] != eng]
+        for k in w:
+            x = st(k)
+            deps += x["w"] + x["r"] + x["b"]
+        for k in p:
+            x = st(k)
+            if x["r"]:
+                x["b"] = x["w"] + x["r"] + x["b"]
+                x["w"], x["r"] = [], []
+            deps += [d for d in x["b"] if not (eng == "t" and d[0] == "t")]
+        kn = known[eng]
+        best = {}
+        for d in deps:
+            if kn.get(d[0], 0) < d[1] and (d[0] not in best or best[d[0]][1] < d[1]):
+                best[d[0]] = d
+        items = list(best.values())
+        for d in items:
+            if any(o is not d and o[2].get(d[0], 0) >= d[1] for o in items):
+                continue
+            if kn.get(d[0], 0) < d[1]:
+                queues[eng].wait_ge(T.sem[d[0]], d[1])
+            for s, n in list(d[2].items()) + [(d[0], d[1])]:
+                if kn.get(s, 0) < n:
+                    kn[s] = n
+
+    def record(ev, r, w, p):
+        for k in r:
+            st(k)["r"].append(ev)
+        for k in w:
+            x = st(k)
+            x["w"], x["r"], x["b"] = [ev], [], [ev]
+        for k in p:
+            st(k)["w"].append(ev)
+
+    def do(eng, fn, r=(), w=(), p=()):
+        waits(eng, r, w, p)
+        count[eng] += 1
+        fn().then_inc(T.sem[eng], 1)
+        record((eng, count[eng], dict(known[eng])), r, w, p)
+
+    def dma(eng, out, in_, r=(), w=(), p=()):
+        waits(eng, r, w, p)
+        s = "d%d" % tally["dma"]
+        tally["dma"] += 1
+        queues[eng].dma_start(out, in_).then_inc(T.sem[s], 16)
+        record((s, 16, dict(known[eng])), r, w, p)
+
+    def engines_between(a, b):
+        return len(topo.engines(a, b))
+
+    def send(dst, rx, out, in_, r):
+        waits("gp", r, (), ())
+        rid, pid, _ = topo.addr(dst)
+        g.remote_dma(out, in_, T.sem["rx%d" % rx], T.sem["ls"], pid, rid, topo.mask(core, dst))
+        tally["ls"] += engines_between(core, dst)
+
+    def send_tile(t, rx, land, name):
+        q = partner(t)
+        send(q, rx, codes(land, 0, NC), codes(name, 0, NC), [name])
+        send(q, rx + 1, T[land + "s"][:, 0:NC], T[name + "s"][:, 0:NC], [name])
+        n = engines_between(q, core)
+        st(land)["w"] = [("rx%d" % rx, n, {}), ("rx%d" % (rx + 1), n, {})]
+
+    def partner(t):
+        return T.cores[rank ^ (1 << t)]
+
+    def codes(name, a, b):
+        return T[name + "c"][:, a:b].bitcast(dt.uint8)
+
+    def bank(k, a=0, b=NC):
+        return T.ps[:, 512 * k + a:512 * k + b]
+
+    def ps(k):
+        return "ps%d" % k
+
+    def plane(name, k, a=0, b=NC):
+        return T[name][:, k * NC + a:k * NC + b]
+
+    def junk(n):
+        k = tally["junk"] % 4
+        tally["junk"] += 1
+        return T.junk[:, 448 * k:448 * k + n], "junk%d" % k
+
+    def quant(name, a, b, tile, ta, r):
+        do("v", lambda: V.quantize_mx(T[name + "c"][:, a:b], T[name + "s"][:, a:b], T[tile][:, ta:ta + 4 * (b - a)]), r=r, p=[name])
+
+    def mm(k, n, left, la, right, ra, start=True, stop=True):
+        kw = {"w": [ps(k)]} if start else {"p": [ps(k)]}
+        do("t", lambda: PE.matmul_mx(bank(k, 0, n), T[left + "c"][:, la:la + 128], T[left + "s"][:, la:la + 128],
+                                     T[right + "c"][:, ra:ra + n], T[right + "s"][:, ra:ra + n], start, stop), r=[left, right], **kw)
+
+    def ts(out, in0, s1, s2, op0, op1=None, **k):
+        if op1 is None:
+            do("v", lambda: V.tensor_scalar(out, in0, s1, s2, op0), **k)
+        else:
+            do("v", lambda: V.tensor_scalar(out, in0, s1, s2, op0, op1), **k)
+
+    def tt(out, a, b, op, **k):
+        do("v", lambda: V.tensor_tensor(out, a, b, op), **k)
+
+    def vcopy(out, in_, **k):
+        do("v", lambda: V.tensor_copy(out, in_), **k)
+
+    def scopy(out, in_, **k):
+        do("s", lambda: S.activation(out, in_, F.Copy), **k)
+
+    def ssum(in_, n, col, key, r):
+        j, jk = junk(n)
+        do("s", lambda: S.activation(j, in_, F.Copy, accum_out=col), r=r, w=[jk], p=[key])
+
+    def scan(out, d0, d1, **k):
+        do("v", lambda: V.tensor_tensor_scan(out, d0, d1, 0.0, A.mult, A.add), **k)
+
+    def fill(ap, c, key):
+        do("v", lambda: V.memset(ap, c), w=[key])
+
+    def iota(name, a, b, pattern, base, cm):
+        ap = T[name][:, a:b]
+        if name == "pi_i":
+            do("gp", lambda: g.iota(ap, pattern, base, cm), p=[name])
+        else:
+            do("gp", lambda: g.iota(ap, pattern, base, cm, allow_small_or_imprecise_dtypes=True), p=[name])
+
+    dma("sy", T.xt0[:, 0:4 * NC], T.x[:, :], p=["xt0"])
+    dma("s", T.ut[:, :], T.u[:, :], w=["ut"])
+    dma("sy", T.xt0[:, 4 * NC:4 * NP], T.x[:, 0:4 * (NP - NC)], p=["xt0"])
+    dma("sy", codes("ww", 0, 1024), T.wc[:, :], p=["ww"])
+    dma("sy", T.wws[:, :], T.ws[:, :], p=["ww"])
+    dma("sy", T.vt[:, :], T.v[:, :], w=["vt"])
+
+    iota("lf", 0, 8, [[16, 8]], 0, 0)
+    iota("lf", 8, 16, [[16, 8]], 1, 0)
+    iota("lf", 16, 24, [[0, 8]], 0, 0)
+    iota("pi_i", 0, 1, [[0, 1]], 0, 1)
+    iota("h8", 0, 8, [[1, 8]], 0, 0)
+    iota("triv", 0, 128, [[1, 128]], 0, -1)
+    iota("tiec", 0, 4, [[-128, 4]], 511, -1)
+    iota("ipr", 0, NC, [[0, NM], [1, 16]], 0, 0)
+    fill(T.nt[:], 0.0, "ntz")
+    fill(T.cb[:, NC:328], -40.0, "cbz")
+    vcopy(T.lu[:], T.lf[:, 0:24], r=["lf"], w=["lu"])
+    ts(T.pi_i[:, 1:2], T.pi_i[:, 0:1], 15, None, A.bitwise_and, r=["pi_i"], w=["pi1"])
+    ts(T.pi_i[:, 2:3], T.pi_i[:, 0:1], 4, None, A.arith_shift_right, r=["pi_i"], w=["pi2"])
+    vcopy(T.pif[:], T.pi_i[:, 1:2], r=["pi1"], w=["pif"])
+    vcopy(T.hcol[:], T.pi_i[:, 2:3], r=["pi2"], w=["hcol"])
+    ts(T.mask8[:], T.h8[:], T.hcol[:, 0:1], None, A.is_equal, r=["h8", "hcol"], w=["mask8"])
+    ts(T.mask8n[:], T.h8[:], T.hcol[:, 0:1], -0.5, A.is_equal, A.mult, r=["h8", "hcol"], w=["mask8n"])
+    ts(T.tri128[:], T.triv[:], 0.0, None, A.is_lt, r=["triv"], w=["tri128"])
+    ts(T.far[:], T.hcol[:], 4.0, 8192.0, A.is_ge, A.mult, r=["hcol"], w=["far"])
+    ts(T.tiec[:], T.tiec[:], 1.0 / 512, 1.0 / 1024, A.mult, A.add, w=["tiec"])
+    tt(T.tiec[:, 2:3], T.tiec[:, 2:3], T.far[:], A.add, r=["far"], w=["tiec"])
+
+    quant("xq0", 0, NP, "xt0", 0, ["xt0"])
+    quant("uq", 0, 128, "ut", 0, ["ut"])
+    do("v", lambda: V.tensor_copy(T.upc[:, 0:384].bitcast(dt.uint32), T.uqc[:, 0:128].bitcast(dt.uint32).indirect(T.lu[:, 0:24])), r=["uq", "lu"], p=["up"])
+    do("s", lambda: S.activation(T.ups[:, 0:384], T.uqs[:, 0:128].indirect(T.lu[:, 0:24]), F.Copy), r=["uq", "lu"], p=["up"])
+    send_tile(0, 0, "px0", "xq0")
+
+    def late_constants():
+        iota("lf", 24, 44, [[16, NM]], 15, 0)
+        iota("bdi", 0, 512, [[0, 8], [1, 16], [0, 4]], 0, 0)
+        iota("tab0", 0, NC, [[-1, NC]], 319, 0)
+        iota("tier", 0, NC, [[-1, NC]], 511, 0)
+        iota("iot", 0, NC, [[1, NC]], 0, 0)
+        ts(T.diag[:], T.ipr[:], T.pif[:, 0:1], None, A.is_equal, r=["ipr", "pif"], w=["diag"])
+        ts(T.rst[:], T.ipr[:], 0.0, None, A.is_gt, r=["ipr"], w=["rst"])
+        ts(T.tri[:], T.ipr[:], T.pif[:, 0:1], None, A.is_lt, r=["ipr", "pif"], w=["tri"])
+        vcopy(T.l15[:], T.lf[:, 24:44], r=["lf"], w=["l15"])
+        ts(T.lm[:], T.lf[:, 24:44], -15.0, 0.0625, A.add, A.mult, r=["lf"], w=["lm"])
+        ts(T.bd[:], T.bdi[:], T.pif[:, 0:1], None, A.is_equal, r=["bdi", "pif"], w=["bd"])
+        quant("kq", KB, KB + 128, "bd", 0, ["bd"])
+        fill(T.bg[:], 0.0, "bg")
+        vcopy(T.bg[:, 448:512], T.bd[:, 0:64], r=["bd"], w=["bg"])
+        quant("kq", KG, KG + 240, "bg", 0, ["bg"])
+
+    def later_constants():
+        ts(T.tier[:], T.tier[:], 1.0 / 512, None, A.mult, w=["tier"])
+        ts(T.ident[:], T.triv[:], 0.0, None, A.is_equal, r=["triv"], w=["ident"])
+        fill(T.et[:], 0.0, "et")
+        for b in range(4):
+            vcopy(T.et[:, 512 * b + b:512 * (b + 1):4], T.ident[:], r=["ident", "et"], w=["et%d" % b])
+        quant("kq", KE, KE + 512, "et", 0, ["et", "et0", "et1", "et2", "et3"])
+        fill(T.ct[:], 0.0, "ct")
+        fill(T.ones[:], 1.0, "ones")
+        for h in range(NG):
+            ts(T.wg[:, 512 * h:512 * h + 512], T.ones[:], T.mask8[:, h:h + 1], None, A.mult, r=["ones", "mask8"], p=["wg"])
+        quant("kq", KW, KW + 512, "wg", 0, ["wg"])
+        quant("kq", KW + 512, KW + 1024, "wg", 2048, ["wg"])
+        quant("vq", 0, 128, "vt", 0, ["vt"])
+
+    def own_places(X):
+        mm(0, NC, "up", 256, X, 0)
+        for c in range(3):
+            mm(1 + c, 128, X, 128 * c, "uq", 0)
+        for c in range(3):
+            o, w = 128 * c, min(128, NC - 128 * c)
+            sc, k, rr = bank(1 + c, 0, 1), 448 * c, [ps(0), ps(1 + c)]
+            key = "a0c%d" % c
+            ts(T.eqb[:, 0:w], bank(0, o, o + w), sc, None, A.is_equal, r=rr, w=["eqb"])
+            if o:
+                ts(T.a0c[:, k:k + o], bank(0, 0, o), sc, None, A.is_ge, r=rr, p=[key])
+            ts(T.a0c[:, k + o:k + NC], bank(0, o, NC), sc, None, A.is_gt, r=rr, p=[key])
+            tt(T.a0c[:, k + NC:k + NC + w], T.eqb[:, 0:w], T.tri128[:, 0:w], A.mult, r=["eqb", "tri128"], p=[key])
+            ssum(T.a0c[:, k:k + NC + w], NC + w, T.a0[:, c:c + 1], "a0", [key])
+
+    def dist(h):
+        ts(T.nt[:, 0:4 * NM:4], T.xn[:, 0:NM], MG16, MG16, A.add, A.subtract, r=["xn", "ntz"], w=["nthi"])
+        tt(T.nt[:, 1:4 * NM:4], T.xn[:, 0:NM], T.nt[:, 0:4 * NM:4], A.subtract, r=["xn", "nthi", "ntz"], w=["ntlo"])
+        do("v", lambda: V.quantize_mx(T.nqc[:, 0:128], T.nqs[:, 0:128], T.nt[:, 0:512]), r=["nthi", "ntlo", "ntz"], w=["nq"])
+        mm(6, 128, "kq", KB, "nq", 0)
+        mm(7, 128, "kq", KG + 112 - 16 * h, "nq", 0, h == 0, h == NG - 1)
+
+    def take_offsets():
+        ts(T.off[:], bank(6, 0, NM), 160.0, None, A.add, r=[ps(6)], w=["off"])
+
+    def score_columns(n, k):
+        tt(T["d" + n][:], bank(k), T.diag[:], A.mult, r=[ps(k), "diag"], w=["d" + n])
+        scan(T["sc" + n][:], T.rst[:], T["d" + n][:], r=["rst", "d" + n], w=["sc" + n])
+        scopy(T["sx" + n][:], T["sc" + n][:, 0:NC].indirect(T.l15[:, 0:NM]), r=["sc" + n, "l15"], w=["sx" + n])
+
+    def group_places(n, k):
+        for m in range(NM):
+            i = tally["ring"] % RING
+            tally["ring"] += 1
+            key = "cmp%d" % i
+            sc = T["sc" + n][:, 16 * m + 15:16 * m + 16]
+            if m:
+                ts(plane("cmp", i, 0, 16 * m), bank(k, 0, 16 * m), sc, None, A.is_ge, r=[ps(k), "sc" + n], p=[key])
+            ts(plane("cmp", i, 16 * m), bank(k, 16 * m), sc, None, A.is_gt, r=[ps(k), "sc" + n], p=[key])
+            ssum(plane("cmp", i), NC, T["acc" + n][:, m:m + 1], "acc" + n, [key])
+        tt(T.eq[:], bank(k), T["sx" + n][:], A.is_equal, r=[ps(k), "sx" + n], w=["eq"])
+        tt(T.tq[:], T.eq[:], T.tri[:], A.mult, r=["eq", "tri"], w=["tq"])
+        scan(T["ee" + n][:], T.rst[:], T.tq[:], r=["rst", "tq"], w=["ee" + n])
+        tt(T["pl" + n][:], T["acc" + n][:], T["ee" + n][:, 15:NC:16], A.add, r=["acc" + n, "ee" + n], w=["pl" + n])
+
+    def table(h):
+        mm(h % 4, NC, "kq", KW + 128 * h, "cq", 0)
+
+    def copy_table(h):
+        k = h % 4
+        if h == 0:
+            tt(plane("cw", 0), bank(k), T.tab0[:], A.add, r=[ps(k), "tab0"], w=["cw0"])
+        else:
+            scopy(plane("cw", h), bank(k), r=[ps(k)], w=["cw%d" % h])
+
+    def count_teams(prev, c):
+        j, jk = junk(NC)
+        do("s", lambda: S.activation(j, T[prev][:], F.Sign, bias=T.pk[:, c:c + 1], scale=-1.0, accum_out=T.cnt[:, c:c + 1]),
+           r=[prev, "pk"], w=["cnt%d" % c, jk])
+
+    def draft_round(t):
+        X, PX, PY, YQ = "xq%d" % t, "px%d" % t, "py%d" % t, "yq%d" % t
+        last = t == 1
+        own_places(X)
+        if t == 0:
+            late_constants()
+        ts(T.d0[:, 0:3], T.a0[:, 0:3], -1.0, 159.0, A.mult, A.add, r=["a0"], w=["d0"])
+        for c in range(3):
+            k = 8 if c < 2 else 4
+            ts(T.xn[:, 8 * c:8 * c + k], T.mask8[:, 0:k], T.d0[:, c:c + 1], None, A.mult, r=["mask8", "d0"], p=["xn"])
+        ts(T.offo[:, 0:3], T.d0[:, 0:3], 160.0, 0.0, A.add, A.max, r=["d0"], w=["offo"])
+        dist(0)
+        if t == 0:
+            later_constants()
+        mm(4, NC, "up", 0, PX, 0)
+        mm(5, NC, "up", 128, PX, 0)
+        take_offsets()
+        score_columns("A", 4)
+        score_columns("B", 5)
+        for b in range(4):
+            k = (6, 0, 1, 2)[b]
+            mm(k, NC, "kq", KE + 128 * b, PX, 0)
+            scopy(plane("fp", b), bank(k), r=[ps(k)], w=["fp%d" % b])
+        group_places("B", 5)
+        scopy(T.bxe[:], T.plB[:, 0:NM].indirect(T.lm[:, 0:NM]), r=["plB", "lm"], w=["bxe"])
+        group_places("A", 4)
+        vcopy(T.aoff[:], T.plA[:], r=["plA"], w=["aoff"])
+        tt(T.bx[:], T.bxe[:], T.diag[:], A.mult, r=["bxe", "diag"], w=["bx"])
+        vcopy(T.cx[:, 0:NC].indirect(T.aoff[:, 0:NM]), T.bx[:], r=["aoff", "bx"], w=["cx"])
+        ts(T.ct[:, 0:4 * NC:4], T.cx[:], MG32, MG32, A.add, A.subtract, r=["cx", "ct"], w=["cthi"])
+        tt(T.ct[:, 1:4 * NC:4], T.cx[:], T.ct[:, 0:4 * NC:4], A.subtract, r=["cx", "cthi", "ct"], w=["ctlo"])
+        quant("cq", 0, NC, "ct", 0, ["cthi", "ctlo", "ct"])
+        for h in range(4):
+            table(h)
+        vcopy(T.ir[:, 0:NC].indirect(T.aoff[:, 0:NM]), T.iot[:], r=["aoff", "iot"], w=["ir"])
+        copy_table(0)
+        copy_table(1)
+        vcopy(T.pk[:, 0:3], T.tiec[:, 0:3], r=["tiec"], w=["pk"])
+        prev = "tier"
+        for h in range(NG):
+            cw = "cw%d" % h
+            if h:
+                for c in range(2):
+                    count_teams(prev, c)
+                ts(T.cb[:, 0:NC], T[prev][:], T.pk[:, 2:3], 2.0, A.is_lt, A.mult, r=[prev, "pk"], w=["cb"])
+                do("v", lambda: V.tensor_reduce(T.cnt[:, 2:3], T.cb[:], AxisListType.X, A.add), r=["cb", "cbz"], w=["cnt2"])
+                for c in (0, 2, 1):
+                    k = 8 if c < 2 else 4
+                    ts(T.xn[:, 8 * c:8 * c + k], T.mask8n[:, 0:k], T.cnt[:, c:c + 1], None, A.mult, r=["mask8n", "cnt%d" % c], p=["xn"])
+                if h < NG - 1:
+                    ts(T.offo[:, 0:3], T.cnt[:, 0:3], -0.5, 160.0, A.mult, A.add, r=["cnt0", "cnt1", "cnt2"], w=["offo"])
+                dist(h)
+            if h < NG - 1:
+                scopy(T.og[:], plane("cw", h).indirect(T.offo[:, 0:3]), r=[cw, "offo"], w=["og"])
+                tt(T.ogd[:], T.og[:], T.diag[:, 0:48], A.mult, r=["og", "diag"], w=["ogd"])
+                scan(T.os1[:], T.rst[:, 0:48], T.ogd[:], r=["rst", "ogd"], w=["os1"])
+                tt(T.pk[:, 0:3], T.pk[:, 0:3], T.os1[:, 15:48:16], A.add, r=["os1"], w=["pk"])
+            if h < NG - 1 or last:
+                if h:
+                    take_offsets()
+                new = "kr%d" % (h % 2)
+                tt(T[new][:], plane("cw", h).indirect(T.off[:, 0:NM]), T[prev][:], A.add, r=[cw, "off", prev], w=[new])
+                prev = new
+            if h == 0:
+                tt(T.di[:], T.ir[:], T.diag[:], A.mult, r=["ir", "diag"], w=["di"])
+                scan(T.si[:], T.rst[:], T.di[:], r=["rst", "di"], w=["si"])
+                vcopy(T.inva[:], T.si[:, 15:NC:16], r=["si"], w=["inva"])
+            if h < 4:
+                table(h + 4)
+            if 1 <= h < NG - 1:
+                copy_table(h + 1)
+            if 1 <= h <= 4:
+                scopy(plane("fs", h - 1), plane("fp", h - 1).indirect(T.inva[:, 0:NM]), r=["fp%d" % (h - 1), "inva"], w=["fs%d" % (h - 1)])
+        ts(T.noff[:], bank(7, 0, NM), 160.0, None, A.add, r=[ps(7)], w=["noff"])
+        for k in range(2):
+            vcopy(T.zt[:, k:4 * NC:4], plane("fs", k).indirect(T.noff[:, 0:NM]), r=["fs%d" % k, "noff"], p=["zt"])
+            j = 2 + k
+            scopy(T.zt[:, j:4 * NC:4], plane("fs", j).indirect(T.noff[:, 0:NM]), r=["fs%d" % j, "noff"], p=["zt"])
+        quant("zq", 0, NC, "zt", 0, ["zt"])
+        for b in range(4):
+            mm(b, NC, "kq", KE + 128 * b, X, 0, True, False)
+        vcopy(T.sr[:, 0:NC].indirect(T.noff[:, 0:NM]), T.iot[:], r=["noff", "iot"], w=["sr"])
+        scopy(T.rk[:], T.sr[:, 0:NC].indirect(T.aoff[:, 0:NM]), r=["sr", "aoff"], w=["rk"])
+        tt(T.rkd[:], T.rk[:], T.diag[:], A.mult, r=["rk", "diag"], w=["rkd"])
+        scan(T.rks[:], T.rst[:], T.rkd[:], r=["rst", "rkd"], w=["rks"])
+        vcopy(T.koff[:], T.rks[:, 15:NC:16], r=["rks"], w=["koff"])
+        for b in range(4):
+            k0, k1, cc = 4 + 2 * (b % 2), 5 + 2 * (b % 2), "cc%d" % (b % 2)
+            mm(k1, NC, "ww", 128 * (b + 4), "zq", 0)
+            mm(k0, NC, "ww", 128 * b, "zq", 0)
+            scopy(T[cc][:], bank(k1), r=[ps(k1)], w=[cc])
+            tt(plane("yp", b), bank(k0), T[cc][:], A.max, r=[ps(k0), cc], w=["yp%d" % b])
+        for k in range(2):
+            do("s", lambda: S.activation(T.yt[:, k:4 * NC:4], plane("yp", k).indirect(T.koff[:, 0:NM]), F.Copy, scale=0.03125), r=["yp%d" % k, "koff"], p=["yt"])
+            j = 2 + k
+            ts(T.yt[:, j:4 * NC:4], plane("yp", j).indirect(T.koff[:, 0:NM]), 0.03125, None, A.mult, r=["yp%d" % j, "koff"], p=["yt"])
+        quant(YQ, 0, NC, "yt", 0, ["yt"])
+        send_tile(t, 4 * t + 2, PY, YQ)
+        if last:
+            tt(T.tsb[0:1, :], T[prev][0:1, :], T.tier[0:1, :], A.subtract, r=[prev, "tier"], w=["tsb"])
+            dma("sy", T.tot[:, :], T.tsb[0:1, :], r=["tsb"])
+        for b in range(4):
+            mm(b, NC, "kq", KE + 128 * b, PY, 0, False, True)
+            cp = scopy if b % 2 else vcopy
+            cp(T.xt1[:, b:4 * NC:4], bank(b), r=[ps(b)], p=["xt1"])
+            if not last:
+                cp(T.xt1[:, 4 * NC + b:4 * NP:4], bank(b, 0, NP - NC), r=[ps(b)], p=["xt1"])
+        quant("xq%d" % (t + 1), 0, NC if last else NP, "xt1", 0, ["xt1"])
+
+    draft_round(0)
+    send_tile(1, 4, "px1", "xq1")
+    draft_round(1)
+
+    mm(4, NC, "vq", 0, "xq2", 0)
+    dma("sy", T.oc[:, :], codes("xq2", 0, NC), r=["xq2"])
+    for k in range(4):
+        dma("sy", T.osc[4 * k:4 * k + 4, :], T.xq2s[32 * k:32 * k + 4, 0:NC], r=["xq2"])
+    scopy(T.ysb[:], bank(4), r=[ps(4)], w=["ysb"])
+    dma("sy", T.y[:, :], T.ysb[:], r=["ysb"])
+
+    for s in ("v", "s", "t", "gp"):
+        g.sync.wait_ge(T.sem[s], count[s])
+    for k in range(tally["dma"]):
+        g.sync.wait_ge(T.sem["d%d" % k], 16)
+    for k in range(8):
+        g.sync.wait_ge(T.sem["rx%d" % k], engines_between(partner(k // 4), core))
+    g.sync.wait_ge(T.sem["ls"], tally["ls"])

@@ -1,10 +1,10 @@
 from concourse.mybir import dt, AluOpType as A, AxisListType, ActivationFunctionType as F
 
 NC = 320
-NP = 384
 NG = 8
 NM = 20
 RING = 6
+PIECE = (0, 128, 192)
 
 F32, BF, I32, U16, FP8, U8 = "float32", "bfloat16", "int32", "uint16", "float8_e4m3fn_x4", "uint8"
 SCRATCH = {"ps": ("psum", [128, 4096], F32)}
@@ -19,16 +19,17 @@ def _mx(name, cols):
     _sb(name + "s", cols, U8)
 
 
-for _n, _c in (("ipr", NC), ("diag", NC), ("rst", NC), ("tab0", NC), ("tier", NC), ("iot", NC), ("hcol", 1), ("pif", 1),
-               ("mask8", 8), ("mask8n", 8), ("h8", 8), ("tiec", 4), ("bdi", 512), ("triv", 128), ("lf", 48), ("far", 1),
+for _n, _c in (("tab0", NC), ("tier", NC), ("iot", NC), ("hcol", 1), ("pif", 1), ("trib", NC),
+               ("mask8", 8), ("mask8n", 8), ("h8", 8), ("tiec", 4), ("triv", 128), ("lf", 48),
                ("a0", 4), ("d0", 4), ("dA", NC), ("dB", NC), ("scA", NC), ("scB", NC), ("sxA", NC), ("sxB", NC),
-               ("accA", NM), ("accB", NM), ("eeA", NC), ("eeB", NC), ("plA", NM), ("plB", NM),
-               ("bxe", NC), ("bx", NC), ("cx", NC), ("ir", NC), ("di", NC), ("si", NC),
-               ("xn", 24), ("kr0", NC), ("kr1", NC), ("pk", 4), ("cnt", 4), ("og", 48), ("ogd", 48), ("os1", 48),
-               ("sr", NC), ("rk", NC), ("rkd", NC), ("rks", NC), ("cc0", NC), ("cc1", NC), ("ysb", NC), ("tsb", NC), ("cw", NG * NC)):
+               ("accA", NM), ("accB", NM), ("plA", NM), ("plB", NM),
+               ("bx", NC), ("cx", NC), ("ir", NC), ("di", NC), ("si", NC),
+               ("xn", 24), ("kr0", NC), ("kr1", NC), ("pk", 4), ("cnt", 4), ("ogd", 48), ("os1", 48),
+               ("sr", NC), ("rkd", NC), ("rks", NC), ("cc", 4 * NC), ("ysb", NC), ("tsb", NC), ("cw", NG * NC)):
     _sb(_n, _c, F32)
-for _n, _c in (("xt0", 4 * NP), ("xt1", 4 * NP), ("ut", 512), ("vt", 512), ("ones", 512), ("ident", 128), ("et", 2048), ("wg", 4096),
-               ("bd", 512), ("bg", 960), ("tri", NC), ("tri128", 128), ("a0c", 3 * 448), ("eqb", 128), ("eq", NC), ("tq", NC),
+for _n, _c in (("ipr", NC), ("diag", NC), ("rst", NC), ("bdi", 512), ("xt0", 4 * NC), ("xt1", 4 * NC), ("ut", 512), ("vt", 512),
+               ("ones", 512), ("ident", 128), ("et", 2048), ("wg", 4096), ("bd", 512), ("bg", 960), ("tri128", 128),
+               ("a0c", 3 * 448), ("eqb", 128), ("eq", NC), ("eeA", NC), ("eeB", NC),
                ("junk", 4 * 448), ("cb", 328), ("ct", 4 * NC), ("nt", 512), ("zt", 4 * NC), ("yt", 4 * NC),
                ("cmp", RING * NC), ("fp", 4 * NC), ("fs", 4 * NC), ("yp", 4 * NC)):
     _sb(_n, _c, BF)
@@ -36,7 +37,7 @@ _sb("pi_i", 4, I32)
 for _n, _c in (("l15", NM), ("lm", NM), ("lu", 24), ("aoff", NM), ("inva", NM), ("off", NM), ("offo", 4), ("noff", NM), ("koff", NM)):
     _sb(_n, _c, U16)
 KE, KW, KB, KG = 0, 512, 1536, 1664
-for _n, _c in (("xq0", NP), ("xq1", NP), ("xq2", NC), ("px0", NC), ("px1", NC), ("py0", NC), ("py1", NC), ("uq", 128), ("up", 384), ("vq", 128),
+for _n, _c in (("xq0", NC), ("xq1", NC), ("xq2", NC), ("px0", NC), ("px1", NC), ("py0", NC), ("py1", NC), ("uq", 128), ("up", 384), ("vq", 128),
                ("kq", 1904), ("nq", 128), ("cq", NC), ("zq", NC), ("yq0", NC), ("yq1", NC), ("ww", 1024)):
     _mx(_n, _c)
 
@@ -171,15 +172,15 @@ def rank_program(g, core, T, topo):
     def vcopy(out, in_, **k):
         do("v", lambda: V.tensor_copy(out, in_), **k)
 
-    def scopy(out, in_, **k):
-        do("s", lambda: S.activation(out, in_, F.Copy), **k)
+    def scopy(out, in_, scale=1.0, **k):
+        do("s", lambda: S.activation(out, in_, F.Copy, scale=scale), **k)
 
     def ssum(in_, n, col, key, r):
         j, jk = junk(n)
         do("s", lambda: S.activation(j, in_, F.Copy, accum_out=col), r=r, w=[jk], p=[key])
 
-    def scan(out, d0, d1, **k):
-        do("v", lambda: V.tensor_tensor_scan(out, d0, d1, 0.0, A.mult, A.add), **k)
+    def scan(out, d1, n=NC, **k):
+        do("v", lambda: V.tensor_tensor_scan(out, T.rst[:, 0:n], d1, 0.0, A.mult, A.add), **k)
 
     def fill(ap, c, key):
         do("v", lambda: V.memset(ap, c), w=[key])
@@ -191,9 +192,8 @@ def rank_program(g, core, T, topo):
         else:
             do("gp", lambda: g.iota(ap, pattern, base, cm, allow_small_or_imprecise_dtypes=True), p=[name])
 
-    dma("sy", T.xt0[:, 0:4 * NC], T.x[:, :], p=["xt0"])
+    dma("sy", T.xt0[:, :], T.x[:, :], p=["xt0"])
     dma("s", T.ut[:, :], T.u[:, :], w=["ut"])
-    dma("sy", T.xt0[:, 4 * NC:4 * NP], T.x[:, 0:4 * (NP - NC)], p=["xt0"])
     dma("sy", codes("ww", 0, 1024), T.wc[:, :], p=["ww"])
     dma("sy", T.wws[:, :], T.ws[:, :], p=["ww"])
     dma("sy", T.vt[:, :], T.v[:, :], w=["vt"])
@@ -201,80 +201,79 @@ def rank_program(g, core, T, topo):
     iota("lf", 0, 8, [[16, 8]], 0, 0)
     iota("lf", 8, 16, [[16, 8]], 1, 0)
     iota("lf", 16, 24, [[0, 8]], 0, 0)
+    iota("triv", 0, 128, [[1, 128]], 0, -1)
     iota("pi_i", 0, 1, [[0, 1]], 0, 1)
     iota("h8", 0, 8, [[1, 8]], 0, 0)
-    iota("triv", 0, 128, [[1, 128]], 0, -1)
-    iota("tiec", 0, 4, [[-128, 4]], 511, -1)
-    iota("ipr", 0, NC, [[0, NM], [1, 16]], 0, 0)
+    iota("tiec", 0, 2, [[-128, 2]], 511, -1)
+    iota("tiec", 2, 3, [[0, 1]], 511 - PIECE[2], -1)
+    fill(T.et[:], 0.0, "et")
+    fill(T.ones[:], 1.0, "ones")
     fill(T.nt[:], 0.0, "ntz")
-    fill(T.cb[:, NC:328], -40.0, "cbz")
     vcopy(T.lu[:], T.lf[:, 0:24], r=["lf"], w=["lu"])
-    ts(T.pi_i[:, 1:2], T.pi_i[:, 0:1], 15, None, A.bitwise_and, r=["pi_i"], w=["pi1"])
-    ts(T.pi_i[:, 2:3], T.pi_i[:, 0:1], 4, None, A.arith_shift_right, r=["pi_i"], w=["pi2"])
-    vcopy(T.pif[:], T.pi_i[:, 1:2], r=["pi1"], w=["pif"])
-    vcopy(T.hcol[:], T.pi_i[:, 2:3], r=["pi2"], w=["hcol"])
-    ts(T.mask8[:], T.h8[:], T.hcol[:, 0:1], None, A.is_equal, r=["h8", "hcol"], w=["mask8"])
-    ts(T.mask8n[:], T.h8[:], T.hcol[:, 0:1], -0.5, A.is_equal, A.mult, r=["h8", "hcol"], w=["mask8n"])
     ts(T.tri128[:], T.triv[:], 0.0, None, A.is_lt, r=["triv"], w=["tri128"])
-    ts(T.far[:], T.hcol[:], 4.0, 8192.0, A.is_ge, A.mult, r=["hcol"], w=["far"])
-    ts(T.tiec[:], T.tiec[:], 1.0 / 512, 1.0 / 1024, A.mult, A.add, w=["tiec"])
-    tt(T.tiec[:, 2:3], T.tiec[:, 2:3], T.far[:], A.add, r=["far"], w=["tiec"])
+    ts(T.ident[:], T.triv[:], 0.0, None, A.is_equal, r=["triv"], w=["ident"])
+    fill(T.cb[:, NC:328], -40.0, "cbz")
 
-    quant("xq0", 0, NP, "xt0", 0, ["xt0"])
+    quant("xq0", 0, NC, "xt0", 0, ["xt0"])
     quant("uq", 0, 128, "ut", 0, ["ut"])
     do("v", lambda: V.tensor_copy(T.upc[:, 0:384].bitcast(dt.uint32), T.uqc[:, 0:128].bitcast(dt.uint32).indirect(T.lu[:, 0:24])), r=["uq", "lu"], p=["up"])
     do("s", lambda: S.activation(T.ups[:, 0:384], T.uqs[:, 0:128].indirect(T.lu[:, 0:24]), F.Copy), r=["uq", "lu"], p=["up"])
     send_tile(0, 0, "px0", "xq0")
 
-    def late_constants():
-        iota("lf", 24, 44, [[16, NM]], 15, 0)
+    def early_constants():
+        iota("ipr", 0, NC, [[0, NM], [1, 16]], 0, 0)
         iota("bdi", 0, 512, [[0, 8], [1, 16], [0, 4]], 0, 0)
-        iota("tab0", 0, NC, [[-1, NC]], 319, 0)
+        iota("lf", 24, 44, [[16, NM]], 15, 0)
         iota("tier", 0, NC, [[-1, NC]], 511, 0)
+        iota("tab0", 0, NC, [[-1, NC]], 319, 0)
         iota("iot", 0, NC, [[1, NC]], 0, 0)
+        ts(T.pi_i[:, 1:2], T.pi_i[:, 0:1], 15, None, A.bitwise_and, r=["pi_i"], w=["pi1"])
+        ts(T.pi_i[:, 2:3], T.pi_i[:, 0:1], 4, None, A.arith_shift_right, r=["pi_i"], w=["pi2"])
+        ts(T.tiec[:, 0:3], T.tiec[:, 0:3], 1.0 / 512, 1.0 / 1024, A.mult, A.add, w=["tiec"])
+        vcopy(T.hcol[:], T.pi_i[:, 2:3], r=["pi2"], w=["hcol"])
+        vcopy(T.pif[:], T.pi_i[:, 1:2], r=["pi1"], w=["pif"])
+        ts(T.mask8[:], T.h8[:], T.hcol[:, 0:1], None, A.is_equal, r=["h8", "hcol"], w=["mask8"])
+        ts(T.mask8n[:], T.h8[:], T.hcol[:, 0:1], -0.5, A.is_equal, A.mult, r=["h8", "hcol"], w=["mask8n"])
+        for b in range(4):
+            scopy(T.et[:, 512 * b + b:512 * (b + 1):4], T.ident[:], r=["ident", "et"], w=["et%d" % b])
+
+    def middle_constants():
+        for h in range(NG):
+            key = "wg%d" % (h // 4)
+            scopy(T.wg[:, 512 * h:512 * h + 512], T.ones[:], T.mask8[:, h:h + 1], r=["ones", "mask8"], p=[key])
+        scopy(T.tier[:], T.tier[:], 1.0 / 512, w=["tier"])
         ts(T.diag[:], T.ipr[:], T.pif[:, 0:1], None, A.is_equal, r=["ipr", "pif"], w=["diag"])
         ts(T.rst[:], T.ipr[:], 0.0, None, A.is_gt, r=["ipr"], w=["rst"])
-        ts(T.tri[:], T.ipr[:], T.pif[:, 0:1], None, A.is_lt, r=["ipr", "pif"], w=["tri"])
-        vcopy(T.l15[:], T.lf[:, 24:44], r=["lf"], w=["l15"])
-        ts(T.lm[:], T.lf[:, 24:44], -15.0, 0.0625, A.add, A.mult, r=["lf"], w=["lm"])
         ts(T.bd[:], T.bdi[:], T.pif[:, 0:1], None, A.is_equal, r=["bdi", "pif"], w=["bd"])
-        quant("kq", KB, KB + 128, "bd", 0, ["bd"])
         fill(T.bg[:], 0.0, "bg")
+        quant("kq", KB, KB + 128, "bd", 0, ["bd"])
         vcopy(T.bg[:, 448:512], T.bd[:, 0:64], r=["bd"], w=["bg"])
+        vcopy(T.l15[:], T.lf[:, 24:44], r=["lf"], w=["l15"])
         quant("kq", KG, KG + 240, "bg", 0, ["bg"])
-
-    def later_constants():
-        ts(T.tier[:], T.tier[:], 1.0 / 512, None, A.mult, w=["tier"])
-        ts(T.ident[:], T.triv[:], 0.0, None, A.is_equal, r=["triv"], w=["ident"])
-        fill(T.et[:], 0.0, "et")
-        for b in range(4):
-            vcopy(T.et[:, 512 * b + b:512 * (b + 1):4], T.ident[:], r=["ident", "et"], w=["et%d" % b])
-        quant("kq", KE, KE + 512, "et", 0, ["et", "et0", "et1", "et2", "et3"])
-        fill(T.ct[:], 0.0, "ct")
-        fill(T.ones[:], 1.0, "ones")
-        for h in range(NG):
-            ts(T.wg[:, 512 * h:512 * h + 512], T.ones[:], T.mask8[:, h:h + 1], None, A.mult, r=["ones", "mask8"], p=["wg"])
-        quant("kq", KW, KW + 512, "wg", 0, ["wg"])
-        quant("kq", KW + 512, KW + 1024, "wg", 2048, ["wg"])
-        quant("vq", 0, 128, "vt", 0, ["vt"])
+        ts(T.lm[:], T.lf[:, 24:44], -15.0, 0.0625, A.add, A.mult, r=["lf"], w=["lm"])
+        ts(T.trib[:], T.ipr[:], T.pif[:, 0:1], 1e29, A.is_ge, A.mult, r=["ipr", "pif"], w=["trib"])
 
     def own_places(X):
         mm(0, NC, "up", 256, X, 0)
         for c in range(3):
-            mm(1 + c, 128, X, 128 * c, "uq", 0)
+            mm(1 + c, 128, X, PIECE[c], "uq", 0)
         for c in range(3):
-            o, w = 128 * c, min(128, NC - 128 * c)
-            sc, k, rr = bank(1 + c, 0, 1), 448 * c, [ps(0), ps(1 + c)]
+            o, sc, k, rr = PIECE[c], bank(1 + c, 0, 1), 448 * c, [ps(0), ps(1 + c)]
             key = "a0c%d" % c
-            ts(T.eqb[:, 0:w], bank(0, o, o + w), sc, None, A.is_equal, r=rr, w=["eqb"])
+            ts(T.eqb[:], bank(0, o, o + 128), sc, None, A.is_equal, r=rr, w=["eqb"])
             if o:
                 ts(T.a0c[:, k:k + o], bank(0, 0, o), sc, None, A.is_ge, r=rr, p=[key])
             ts(T.a0c[:, k + o:k + NC], bank(0, o, NC), sc, None, A.is_gt, r=rr, p=[key])
-            tt(T.a0c[:, k + NC:k + NC + w], T.eqb[:, 0:w], T.tri128[:, 0:w], A.mult, r=["eqb", "tri128"], p=[key])
-            ssum(T.a0c[:, k:k + NC + w], NC + w, T.a0[:, c:c + 1], "a0", [key])
+            tt(T.a0c[:, k + NC:k + NC + 128], T.eqb[:], T.tri128[:], A.mult, r=["eqb", "tri128"], p=[key])
+            ssum(T.a0c[:, k:k + 448], 448, T.a0[:, c:c + 1], "a0", [key])
 
-    def dist(h):
+    def block_of(c):
+        return (8 * c, 8 * c + 8, 0, 8) if c < 2 else (16, 20, 4, 8)
+
+    def digits_high():
         ts(T.nt[:, 0:4 * NM:4], T.xn[:, 0:NM], MG16, MG16, A.add, A.subtract, r=["xn", "ntz"], w=["nthi"])
+
+    def digits_low_and_spread(h):
         tt(T.nt[:, 1:4 * NM:4], T.xn[:, 0:NM], T.nt[:, 0:4 * NM:4], A.subtract, r=["xn", "nthi", "ntz"], w=["ntlo"])
         do("v", lambda: V.quantize_mx(T.nqc[:, 0:128], T.nqs[:, 0:128], T.nt[:, 0:512]), r=["nthi", "ntlo", "ntz"], w=["nq"])
         mm(6, 128, "kq", KB, "nq", 0)
@@ -285,8 +284,7 @@ def rank_program(g, core, T, topo):
 
     def score_columns(n, k):
         tt(T["d" + n][:], bank(k), T.diag[:], A.mult, r=[ps(k), "diag"], w=["d" + n])
-        scan(T["sc" + n][:], T.rst[:], T["d" + n][:], r=["rst", "d" + n], w=["sc" + n])
-        scopy(T["sx" + n][:], T["sc" + n][:, 0:NC].indirect(T.l15[:, 0:NM]), r=["sc" + n, "l15"], w=["sx" + n])
+        scan(T["sc" + n][:], T["d" + n][:], r=["rst", "d" + n], w=["sc" + n])
 
     def group_places(n, k):
         for m in range(NM):
@@ -298,9 +296,9 @@ def rank_program(g, core, T, topo):
                 ts(plane("cmp", i, 0, 16 * m), bank(k, 0, 16 * m), sc, None, A.is_ge, r=[ps(k), "sc" + n], p=[key])
             ts(plane("cmp", i, 16 * m), bank(k, 16 * m), sc, None, A.is_gt, r=[ps(k), "sc" + n], p=[key])
             ssum(plane("cmp", i), NC, T["acc" + n][:, m:m + 1], "acc" + n, [key])
+        tt(T["sx" + n][:], T["sc" + n][:, 0:NC].indirect(T.l15[:, 0:NM]), T.trib[:], A.add, r=["sc" + n, "l15", "trib"], w=["sx" + n])
         tt(T.eq[:], bank(k), T["sx" + n][:], A.is_equal, r=[ps(k), "sx" + n], w=["eq"])
-        tt(T.tq[:], T.eq[:], T.tri[:], A.mult, r=["eq", "tri"], w=["tq"])
-        scan(T["ee" + n][:], T.rst[:], T.tq[:], r=["rst", "tq"], w=["ee" + n])
+        scan(T["ee" + n][:], T.eq[:], r=["rst", "eq"], w=["ee" + n])
         tt(T["pl" + n][:], T["acc" + n][:], T["ee" + n][:, 15:NC:16], A.add, r=["acc" + n, "ee" + n], w=["pl" + n])
 
     def table(h):
@@ -321,76 +319,88 @@ def rank_program(g, core, T, topo):
     def draft_round(t):
         X, PX, PY, YQ = "xq%d" % t, "px%d" % t, "py%d" % t, "yq%d" % t
         last = t == 1
+        if t == 0:
+            early_constants()
         own_places(X)
         if t == 0:
-            late_constants()
+            middle_constants()
         ts(T.d0[:, 0:3], T.a0[:, 0:3], -1.0, 159.0, A.mult, A.add, r=["a0"], w=["d0"])
         for c in range(3):
-            k = 8 if c < 2 else 4
-            ts(T.xn[:, 8 * c:8 * c + k], T.mask8[:, 0:k], T.d0[:, c:c + 1], None, A.mult, r=["mask8", "d0"], p=["xn"])
-        ts(T.offo[:, 0:3], T.d0[:, 0:3], 160.0, 0.0, A.add, A.max, r=["d0"], w=["offo"])
-        dist(0)
+            a, b, ma, mb = block_of(c)
+            ts(T.xn[:, a:b], T.mask8[:, ma:mb], T.d0[:, c:c + 1], None, A.mult, r=["mask8", "d0"], p=["xn"])
+        digits_high()
+        ts(T.offo[:, 0:3], T.d0[:, 0:3], 160.0, None, A.add, r=["d0"], w=["offo"])
+        digits_low_and_spread(0)
         if t == 0:
-            later_constants()
-        mm(4, NC, "up", 0, PX, 0)
+            quant("kq", KE, KE + 512, "et", 0, ["et", "et0", "et1", "et2", "et3"])
+            fill(T.ct[:], 0.0, "ct")
         mm(5, NC, "up", 128, PX, 0)
+        mm(4, NC, "up", 0, PX, 0)
         take_offsets()
-        score_columns("A", 4)
         score_columns("B", 5)
+        score_columns("A", 4)
         for b in range(4):
             k = (6, 0, 1, 2)[b]
             mm(k, NC, "kq", KE + 128 * b, PX, 0)
             scopy(plane("fp", b), bank(k), r=[ps(k)], w=["fp%d" % b])
         group_places("B", 5)
-        scopy(T.bxe[:], T.plB[:, 0:NM].indirect(T.lm[:, 0:NM]), r=["plB", "lm"], w=["bxe"])
+        if t == 0:
+            quant("kq", KW, KW + 512, "wg", 0, ["wg0"])
+            quant("kq", KW + 512, KW + 1024, "wg", 2048, ["wg1"])
         group_places("A", 4)
+        tt(T.bx[:], T.plB[:, 0:NM].indirect(T.lm[:, 0:NM]), T.diag[:], A.mult, r=["plB", "lm", "diag"], w=["bx"])
         vcopy(T.aoff[:], T.plA[:], r=["plA"], w=["aoff"])
-        tt(T.bx[:], T.bxe[:], T.diag[:], A.mult, r=["bxe", "diag"], w=["bx"])
         vcopy(T.cx[:, 0:NC].indirect(T.aoff[:, 0:NM]), T.bx[:], r=["aoff", "bx"], w=["cx"])
         ts(T.ct[:, 0:4 * NC:4], T.cx[:], MG32, MG32, A.add, A.subtract, r=["cx", "ct"], w=["cthi"])
         tt(T.ct[:, 1:4 * NC:4], T.cx[:], T.ct[:, 0:4 * NC:4], A.subtract, r=["cx", "cthi", "ct"], w=["ctlo"])
         quant("cq", 0, NC, "ct", 0, ["cthi", "ctlo", "ct"])
         for h in range(4):
             table(h)
-        vcopy(T.ir[:, 0:NC].indirect(T.aoff[:, 0:NM]), T.iot[:], r=["aoff", "iot"], w=["ir"])
+        vcopy(T.pk[:, 0:3], T.tiec[:, 0:3], r=["tiec"], w=["pk"])
         copy_table(0)
         copy_table(1)
-        vcopy(T.pk[:, 0:3], T.tiec[:, 0:3], r=["tiec"], w=["pk"])
         prev = "tier"
         for h in range(NG):
-            cw = "cw%d" % h
+            cw, own, row = "cw%d" % h, h < NG - 1, h < NG - 1 or last
             if h:
-                for c in range(2):
+                ns = 3 if h < 3 else 2
+                for c in range(ns):
                     count_teams(prev, c)
-                ts(T.cb[:, 0:NC], T[prev][:], T.pk[:, 2:3], 2.0, A.is_lt, A.mult, r=[prev, "pk"], w=["cb"])
-                do("v", lambda: V.tensor_reduce(T.cnt[:, 2:3], T.cb[:], AxisListType.X, A.add), r=["cb", "cbz"], w=["cnt2"])
-                for c in (0, 2, 1):
-                    k = 8 if c < 2 else 4
-                    ts(T.xn[:, 8 * c:8 * c + k], T.mask8n[:, 0:k], T.cnt[:, c:c + 1], None, A.mult, r=["mask8n", "cnt%d" % c], p=["xn"])
-                if h < NG - 1:
+                for c in range(ns):
+                    a, b, ma, mb = block_of(c)
+                    scopy(T.xn[:, a:b], T.mask8n[:, ma:mb], T.cnt[:, c:c + 1], r=["mask8n", "cnt%d" % c], p=["xn"])
+                if h == 1:
+                    vcopy(T.ir[:, 0:NC].indirect(T.aoff[:, 0:NM]), T.iot[:], r=["aoff", "iot"], w=["ir"])
+                elif h == 2:
+                    tt(T.di[:], T.ir[:], T.diag[:], A.mult, r=["ir", "diag"], w=["di"])
+                    scan(T.si[:], T.di[:], r=["rst", "di"], w=["si"])
+                    vcopy(T.inva[:], T.si[:, 15:NC:16], r=["si"], w=["inva"])
+                else:
+                    ts(T.cb[:, 0:NC], T[prev][:], T.pk[:, 2:3], 2.0, A.is_lt, A.mult, r=[prev, "pk"], w=["cb"])
+                    do("v", lambda: V.tensor_reduce(T.cnt[:, 2:3], T.cb[:], AxisListType.X, A.add), r=["cb", "cbz"], w=["cnt2"])
+                    a, b, ma, mb = block_of(2)
+                    ts(T.xn[:, a:b], T.mask8n[:, ma:mb], T.cnt[:, 2:3], None, A.mult, r=["mask8n", "cnt2"], p=["xn"])
+                digits_high()
+                if own:
                     ts(T.offo[:, 0:3], T.cnt[:, 0:3], -0.5, 160.0, A.mult, A.add, r=["cnt0", "cnt1", "cnt2"], w=["offo"])
-                dist(h)
-            if h < NG - 1:
-                scopy(T.og[:], plane("cw", h).indirect(T.offo[:, 0:3]), r=[cw, "offo"], w=["og"])
-                tt(T.ogd[:], T.og[:], T.diag[:, 0:48], A.mult, r=["og", "diag"], w=["ogd"])
-                scan(T.os1[:], T.rst[:, 0:48], T.ogd[:], r=["rst", "ogd"], w=["os1"])
+                digits_low_and_spread(h)
+            if own:
+                tt(T.ogd[:], plane("cw", h).indirect(T.offo[:, 0:3]), T.diag[:, 0:48], A.mult, r=[cw, "offo", "diag"], w=["ogd"])
+                scan(T.os1[:], T.ogd[:], 48, r=["rst", "ogd"], w=["os1"])
+            if h and row:
+                take_offsets()
+            if own:
                 tt(T.pk[:, 0:3], T.pk[:, 0:3], T.os1[:, 15:48:16], A.add, r=["os1"], w=["pk"])
-            if h < NG - 1 or last:
-                if h:
-                    take_offsets()
+            if row:
                 new = "kr%d" % (h % 2)
                 tt(T[new][:], plane("cw", h).indirect(T.off[:, 0:NM]), T[prev][:], A.add, r=[cw, "off", prev], w=[new])
                 prev = new
-            if h == 0:
-                tt(T.di[:], T.ir[:], T.diag[:], A.mult, r=["ir", "diag"], w=["di"])
-                scan(T.si[:], T.rst[:], T.di[:], r=["rst", "di"], w=["si"])
-                vcopy(T.inva[:], T.si[:, 15:NC:16], r=["si"], w=["inva"])
             if h < 4:
                 table(h + 4)
             if 1 <= h < NG - 1:
                 copy_table(h + 1)
-            if 1 <= h <= 4:
-                scopy(plane("fs", h - 1), plane("fp", h - 1).indirect(T.inva[:, 0:NM]), r=["fp%d" % (h - 1), "inva"], w=["fs%d" % (h - 1)])
+            if 3 <= h <= 6:
+                scopy(plane("fs", h - 3), plane("fp", h - 3).indirect(T.inva[:, 0:NM]), r=["fp%d" % (h - 3), "inva"], w=["fs%d" % (h - 3)])
         ts(T.noff[:], bank(7, 0, NM), 160.0, None, A.add, r=[ps(7)], w=["noff"])
         for k in range(2):
             vcopy(T.zt[:, k:4 * NC:4], plane("fs", k).indirect(T.noff[:, 0:NM]), r=["fs%d" % k, "noff"], p=["zt"])
@@ -398,20 +408,23 @@ def rank_program(g, core, T, topo):
             scopy(T.zt[:, j:4 * NC:4], plane("fs", j).indirect(T.noff[:, 0:NM]), r=["fs%d" % j, "noff"], p=["zt"])
         quant("zq", 0, NC, "zt", 0, ["zt"])
         for b in range(4):
-            mm(b, NC, "kq", KE + 128 * b, X, 0, True, False)
+            mm(4 + b, NC, "ww", 128 * (b + 4), "zq", 0)
+            mm(b, NC, "ww", 128 * b, "zq", 0)
+            scopy(plane("cc", b), bank(4 + b), r=[ps(4 + b)], w=["cc%d" % b])
+
+        def larger(b):
+            tt(plane("yp", b), bank(b), plane("cc", b), A.max, r=[ps(b), "cc%d" % b], w=["yp%d" % b])
+
         vcopy(T.sr[:, 0:NC].indirect(T.noff[:, 0:NM]), T.iot[:], r=["noff", "iot"], w=["sr"])
-        scopy(T.rk[:], T.sr[:, 0:NC].indirect(T.aoff[:, 0:NM]), r=["sr", "aoff"], w=["rk"])
-        tt(T.rkd[:], T.rk[:], T.diag[:], A.mult, r=["rk", "diag"], w=["rkd"])
-        scan(T.rks[:], T.rst[:], T.rkd[:], r=["rst", "rkd"], w=["rks"])
+        larger(0)
+        tt(T.rkd[:], T.sr[:, 0:NC].indirect(T.aoff[:, 0:NM]), T.diag[:], A.mult, r=["sr", "aoff", "diag"], w=["rkd"])
+        larger(1)
+        scan(T.rks[:], T.rkd[:], r=["rst", "rkd"], w=["rks"])
+        larger(2)
         vcopy(T.koff[:], T.rks[:, 15:NC:16], r=["rks"], w=["koff"])
-        for b in range(4):
-            k0, k1, cc = 4 + 2 * (b % 2), 5 + 2 * (b % 2), "cc%d" % (b % 2)
-            mm(k1, NC, "ww", 128 * (b + 4), "zq", 0)
-            mm(k0, NC, "ww", 128 * b, "zq", 0)
-            scopy(T[cc][:], bank(k1), r=[ps(k1)], w=[cc])
-            tt(plane("yp", b), bank(k0), T[cc][:], A.max, r=[ps(k0), cc], w=["yp%d" % b])
+        larger(3)
         for k in range(2):
-            do("s", lambda: S.activation(T.yt[:, k:4 * NC:4], plane("yp", k).indirect(T.koff[:, 0:NM]), F.Copy, scale=0.03125), r=["yp%d" % k, "koff"], p=["yt"])
+            scopy(T.yt[:, k:4 * NC:4], plane("yp", k).indirect(T.koff[:, 0:NM]), 0.03125, r=["yp%d" % k, "koff"], p=["yt"])
             j = 2 + k
             ts(T.yt[:, j:4 * NC:4], plane("yp", j).indirect(T.koff[:, 0:NM]), 0.03125, None, A.mult, r=["yp%d" % j, "koff"], p=["yt"])
         quant(YQ, 0, NC, "yt", 0, ["yt"])
@@ -419,13 +432,15 @@ def rank_program(g, core, T, topo):
         if last:
             tt(T.tsb[0:1, :], T[prev][0:1, :], T.tier[0:1, :], A.subtract, r=[prev, "tier"], w=["tsb"])
             dma("sy", T.tot[:, :], T.tsb[0:1, :], r=["tsb"])
+        else:
+            quant("vq", 0, 128, "vt", 0, ["vt"])
+        for b in range(4):
+            mm(b, NC, "kq", KE + 128 * b, X, 0, True, False)
         for b in range(4):
             mm(b, NC, "kq", KE + 128 * b, PY, 0, False, True)
             cp = scopy if b % 2 else vcopy
             cp(T.xt1[:, b:4 * NC:4], bank(b), r=[ps(b)], p=["xt1"])
-            if not last:
-                cp(T.xt1[:, 4 * NC + b:4 * NP:4], bank(b, 0, NP - NC), r=[ps(b)], p=["xt1"])
-        quant("xq%d" % (t + 1), 0, NC if last else NP, "xt1", 0, ["xt1"])
+        quant("xq%d" % (t + 1), 0, NC, "xt1", 0, ["xt1"])
 
     draft_round(0)
     send_tile(1, 4, "px1", "xq1")
@@ -436,7 +451,7 @@ def rank_program(g, core, T, topo):
     for k in range(4):
         dma("sy", T.osc[4 * k:4 * k + 4, :], T.xq2s[32 * k:32 * k + 4, 0:NC], r=["xq2"])
     scopy(T.ysb[:], bank(4), r=[ps(4)], w=["ysb"])
-    dma("sy", T.y[:, :], T.ysb[:], r=["ysb"])
+    dma("s", T.y[:, :], T.ysb[:], r=["ysb"])
 
     for s in ("v", "s", "t", "gp"):
         g.sync.wait_ge(T.sem[s], count[s])

@@ -3,7 +3,8 @@ from concourse.mybir import dt, AluOpType as A, AxisListType, ActivationFunction
 NC = 320
 NG = 8
 NM = 20
-RING = 6
+TILE = ((0, 128), (128, 128), (256, 192), (448, 320), (768, 320))
+BY_VECTOR, BY_SCALAR = (4, 1, 0), (2, 3)
 PIECE = (0, 128, 192)
 
 F32, BF, I32, U16, FP8, U8 = "float32", "bfloat16", "int32", "uint16", "float8_e4m3fn_x4", "uint8"
@@ -19,26 +20,26 @@ def _mx(name, cols):
     _sb(name + "s", cols, U8)
 
 
-for _n, _c in (("tab0", NC), ("tier", NC), ("iot", NC), ("hcol", 1), ("pif", 1), ("trib", NC),
+for _n, _c in (("tab0", NC), ("tier", NC), ("iot", NC), ("hcol", 1), ("pif", 1), ("trib", NC), ("ramp", NM),
                ("mask8", 8), ("mask8n", 8), ("h8", 8), ("tiec", 4), ("triv", 128), ("lf", 48),
-               ("a0", 4), ("d0", 4), ("dA", NC), ("dB", NC), ("scA", NC), ("scB", NC), ("sxA", NC), ("sxB", NC),
-               ("accA", NM), ("accB", NM), ("plA", NM), ("plB", NM),
+               ("a0", 4), ("d0", 4), ("dg", 2 * NC), ("sc", 2 * NC), ("sx", 2 * NC), ("sg", 2 * NC), ("row", 2 * NC), ("cs", 2 * NC),
+               ("accA", NM), ("accB", NM), ("owA", NM), ("owB", NM), ("plA", NM), ("plB", NM),
                ("bx", NC), ("cx", NC), ("ir", NC), ("di", NC), ("si", NC),
                ("xn", 24), ("kr0", NC), ("kr1", NC), ("pk", 4), ("cnt", 4), ("ogd", 48), ("os1", 48),
                ("sr", NC), ("rkd", NC), ("rks", NC), ("cc", 4 * NC), ("ysb", NC), ("tsb", NC), ("cw", NG * NC)):
     _sb(_n, _c, F32)
-for _n, _c in (("ipr", NC), ("diag", NC), ("rst", NC), ("bdi", 512), ("xt0", 4 * NC), ("xt1", 4 * NC), ("ut", 512), ("vt", 512),
-               ("ones", 512), ("ident", 128), ("et", 2048), ("wg", 4096), ("bd", 512), ("bg", 960), ("tri128", 128),
-               ("a0c", 3 * 448), ("eqb", 128), ("eq", NC), ("eeA", NC), ("eeB", NC),
+for _n, _c in (("ipr", NC), ("diag", NC), ("rst", NC), ("bdi", 512), ("gob", 512), ("go", 512), ("xt0", 4 * NC), ("xt1", 4 * NC),
+               ("ut", 512), ("vt", 512), ("ones", 512), ("ident", 128), ("et", 2048), ("wg", 4096), ("bd", 512), ("bg", 960), ("tri128", 128),
+               ("a0c", 3 * 448), ("eqb", 128), ("eq", 2 * NC), ("ee", 2 * NC), ("gt", 2 * NC), ("gg", 2 * NC), ("mtA", 4352), ("mtB", 4352),
                ("junk", 4 * 448), ("cb", 328), ("ct", 4 * NC), ("nt", 512), ("zt", 4 * NC), ("yt", 4 * NC),
-               ("cmp", RING * NC), ("fp", 4 * NC), ("fs", 4 * NC), ("yp", 4 * NC)):
+               ("fp", 4 * NC), ("fs", 4 * NC), ("yp", 4 * NC)):
     _sb(_n, _c, BF)
 _sb("pi_i", 4, I32)
 for _n, _c in (("l15", NM), ("lm", NM), ("lu", 24), ("aoff", NM), ("inva", NM), ("off", NM), ("offo", 4), ("noff", NM), ("koff", NM)):
     _sb(_n, _c, U16)
-KE, KW, KB, KG = 0, 512, 1536, 1664
+KE, KW, KB, KG, KO = 0, 512, 1536, 1664, 1904
 for _n, _c in (("xq0", NC), ("xq1", NC), ("xq2", NC), ("px0", NC), ("px1", NC), ("py0", NC), ("py1", NC), ("uq", 128), ("up", 384), ("vq", 128),
-               ("kq", 1904), ("nq", 128), ("cq", NC), ("zq", NC), ("yq0", NC), ("yq1", NC), ("ww", 1024)):
+               ("kq", 2032), ("mq", 2176), ("nq", 128), ("cq", NC), ("zq", NC), ("yq0", NC), ("yq1", NC), ("ww", 1024)):
     _mx(_n, _c)
 
 SEMAPHORES = ["v", "s", "t", "gp", "ls"] + ["d%d" % k for k in range(16)] + ["rx%d" % k for k in range(8)]
@@ -56,7 +57,7 @@ def rank_program(g, core, T, topo):
     known = {q: {} for q in queues}
     count = {"v": 0, "s": 0, "t": 0, "gp": 0}
     state = {}
-    tally = {"dma": 0, "ls": 0, "ring": 0, "junk": 0}
+    tally = {"dma": 0, "ls": 0, "junk": 0}
 
     def st(k):
         if k not in state:
@@ -147,6 +148,13 @@ def rank_program(g, core, T, topo):
     def plane(name, k, a=0, b=NC):
         return T[name][:, k * NC + a:k * NC + b]
 
+    def half(name, n, a=0, b=NC, step=1):
+        o = NC if n == "B" else 0
+        return T[name][:, o + a:o + b:step]
+
+    def lasts(name, n):
+        return half(name, n, 15, NC, 16)
+
     def junk(n):
         k = tally["junk"] % 4
         tally["junk"] += 1
@@ -155,10 +163,10 @@ def rank_program(g, core, T, topo):
     def quant(name, a, b, tile, ta, r):
         do("v", lambda: V.quantize_mx(T[name + "c"][:, a:b], T[name + "s"][:, a:b], T[tile][:, ta:ta + 4 * (b - a)]), r=r, p=[name])
 
-    def mm(k, n, left, la, right, ra, start=True, stop=True):
+    def mm(k, n, left, la, right, ra, start=True, stop=True, key=None):
         kw = {"w": [ps(k)]} if start else {"p": [ps(k)]}
         do("t", lambda: PE.matmul_mx(bank(k, 0, n), T[left + "c"][:, la:la + 128], T[left + "s"][:, la:la + 128],
-                                     T[right + "c"][:, ra:ra + n], T[right + "s"][:, ra:ra + n], start, stop), r=[left, right], **kw)
+                                     T[right + "c"][:, ra:ra + n], T[right + "s"][:, ra:ra + n], start, stop), r=[left, key or right], **kw)
 
     def ts(out, in0, s1, s2, op0, op1=None, **k):
         if op1 is None:
@@ -206,13 +214,19 @@ def rank_program(g, core, T, topo):
     iota("h8", 0, 8, [[1, 8]], 0, 0)
     iota("tiec", 0, 2, [[-128, 2]], 511, -1)
     iota("tiec", 2, 3, [[0, 1]], 511 - PIECE[2], -1)
-    fill(T.et[:], 0.0, "et")
     fill(T.ones[:], 1.0, "ones")
+    fill(T.et[:], 0.0, "et")
     fill(T.nt[:], 0.0, "ntz")
     vcopy(T.lu[:], T.lf[:, 0:24], r=["lf"], w=["lu"])
     ts(T.tri128[:], T.triv[:], 0.0, None, A.is_lt, r=["triv"], w=["tri128"])
     ts(T.ident[:], T.triv[:], 0.0, None, A.is_equal, r=["triv"], w=["ident"])
     fill(T.cb[:, NC:328], -40.0, "cbz")
+    fill(T.bg[:], 0.0, "bg")
+    for n in "BA":
+        fill(T["acc" + n][:, 0:1], 0.0, "acc0" + n)
+        for u, (o, w) in enumerate(TILE):
+            a, b = 4 * o + 256 * u, 4 * (o + w)
+            scopy(T["mt" + n][:, a:b], T.ones[:, 0:b - a], 0.0, r=["ones"], w=["mz%s%d" % (n, u)])
 
     quant("xq0", 0, NC, "xt0", 0, ["xt0"])
     quant("uq", 0, 128, "ut", 0, ["ut"])
@@ -224,6 +238,7 @@ def rank_program(g, core, T, topo):
         iota("ipr", 0, NC, [[0, NM], [1, 16]], 0, 0)
         iota("bdi", 0, 512, [[0, 8], [1, 16], [0, 4]], 0, 0)
         iota("lf", 24, 44, [[16, NM]], 15, 0)
+        iota("gob", 0, 512, [[1, 8], [0, 64]], 0, 0)
         iota("tier", 0, NC, [[-1, NC]], 511, 0)
         iota("tab0", 0, NC, [[-1, NC]], 319, 0)
         iota("iot", 0, NC, [[1, NC]], 0, 0)
@@ -239,18 +254,19 @@ def rank_program(g, core, T, topo):
 
     def middle_constants():
         for h in range(NG):
-            key = "wg%d" % (h // 4)
-            scopy(T.wg[:, 512 * h:512 * h + 512], T.ones[:], T.mask8[:, h:h + 1], r=["ones", "mask8"], p=[key])
+            scopy(T.wg[:, 512 * h:512 * h + 512], T.ones[:], T.mask8[:, h:h + 1], r=["ones", "mask8"], p=["wg%d" % (h // 4)])
         scopy(T.tier[:], T.tier[:], 1.0 / 512, w=["tier"])
         ts(T.diag[:], T.ipr[:], T.pif[:, 0:1], None, A.is_equal, r=["ipr", "pif"], w=["diag"])
         ts(T.rst[:], T.ipr[:], 0.0, None, A.is_gt, r=["ipr"], w=["rst"])
         ts(T.bd[:], T.bdi[:], T.pif[:, 0:1], None, A.is_equal, r=["bdi", "pif"], w=["bd"])
-        fill(T.bg[:], 0.0, "bg")
+        vcopy(T.l15[:], T.lf[:, 24:44], r=["lf"], w=["l15"])
         quant("kq", KB, KB + 128, "bd", 0, ["bd"])
         vcopy(T.bg[:, 448:512], T.bd[:, 0:64], r=["bd"], w=["bg"])
-        vcopy(T.l15[:], T.lf[:, 24:44], r=["lf"], w=["l15"])
+        ts(T.go[:], T.gob[:], T.hcol[:, 0:1], None, A.is_equal, r=["gob", "hcol"], w=["go"])
         quant("kq", KG, KG + 240, "bg", 0, ["bg"])
         ts(T.lm[:], T.lf[:, 24:44], -15.0, 0.0625, A.add, A.mult, r=["lf"], w=["lm"])
+        ts(T.ramp[:], T.lf[:, 24:44], -15.0, None, A.add, r=["lf"], w=["ramp"])
+        quant("kq", KO, KO + 128, "go", 0, ["go"])
         ts(T.trib[:], T.ipr[:], T.pif[:, 0:1], 1e29, A.is_ge, A.mult, r=["ipr", "pif"], w=["trib"])
 
     def own_places(X):
@@ -283,23 +299,70 @@ def rank_program(g, core, T, topo):
         ts(T.off[:], bank(6, 0, NM), 160.0, None, A.add, r=[ps(6)], w=["off"])
 
     def score_columns(n, k):
-        tt(T["d" + n][:], bank(k), T.diag[:], A.mult, r=[ps(k), "diag"], w=["d" + n])
-        scan(T["sc" + n][:], T["d" + n][:], r=["rst", "d" + n], w=["sc" + n])
+        tt(half("dg", n), bank(k), T.diag[:], A.mult, r=[ps(k), "diag"], w=["dg" + n])
+        scopy(half("row", n), bank(k), r=[ps(k)], w=["row" + n])
+        scan(half("sc", n), half("dg", n), r=["rst", "dg" + n], w=["sc" + n])
 
-    def group_places(n, k):
-        for m in range(NM):
-            i = tally["ring"] % RING
-            tally["ring"] += 1
-            key = "cmp%d" % i
-            sc = T["sc" + n][:, 16 * m + 15:16 * m + 16]
-            if m:
-                ts(plane("cmp", i, 0, 16 * m), bank(k, 0, 16 * m), sc, None, A.is_ge, r=[ps(k), "sc" + n], p=[key])
-            ts(plane("cmp", i, 16 * m), bank(k, 16 * m), sc, None, A.is_gt, r=[ps(k), "sc" + n], p=[key])
-            ssum(plane("cmp", i), NC, T["acc" + n][:, m:m + 1], "acc" + n, [key])
-        tt(T["sx" + n][:], T["sc" + n][:, 0:NC].indirect(T.l15[:, 0:NM]), T.trib[:], A.add, r=["sc" + n, "l15", "trib"], w=["sx" + n])
-        tt(T.eq[:], bank(k), T["sx" + n][:], A.is_equal, r=[ps(k), "sx" + n], w=["eq"])
-        scan(T["ee" + n][:], T.eq[:], r=["rst", "eq"], w=["ee" + n])
-        tt(T["pl" + n][:], T["acc" + n][:], T["ee" + n][:, 15:NC:16], A.add, r=["acc" + n, "ee" + n], w=["pl" + n])
+    def blocks(u):
+        return range(max(1, 4 * u), 4 * u + 4)
+
+    def part(n, m):
+        o, e = 4 * TILE[m // 4][0], m % 4
+        return T["mt" + n][:, o + e:o + 64 * m:4]
+
+    def score(n, m):
+        return half("sc", n, 16 * m + 15, 16 * m + 16)
+
+    def compare(n, k):
+        for u in BY_VECTOR:
+            for m in blocks(u):
+                ts(part(n, m), bank(k, 0, 16 * m), score(n, m), None, A.is_lt, r=[ps(k), "sc" + n, "mz%s%d" % (n, u)], w=["mt%s%d" % (n, m)])
+
+    def scalar_compare(n):
+        late = None
+        for m in [m for u in BY_SCALAR for m in blocks(u)] + [None]:
+            if m is not None:
+                j, jk = junk(16 * m)
+                do("s", lambda: S.activation(j, half("row", n, 0, 16 * m), F.Sign, bias=score(n, m), scale=-1.0), r=["row" + n, "sc" + n], w=[jk])
+            if late:
+                q, i, ik = late
+                do("s", lambda: S.activation(part(n, q), i, F.Relu, accum_out=T["acc" + n][:, q:q + 1]),
+                   r=[ik, "mz%s%d" % (n, q // 4)], w=["mt%s%d" % (n, q)], p=["acc" + n])
+            late = (m, j, jk)
+
+    def add_up(n):
+        for u in BY_VECTOR:
+            for m in blocks(u):
+                ssum(part(n, m), 16 * m, T["acc" + n][:, m:m + 1], "acc" + n, ["mt%s%d" % (n, m)])
+
+    def tile_sums(n, us, to):
+        for u in us:
+            (o, w), key = TILE[u], "mq%s%d" % (n, u)
+            c = o + (1088 if n == "B" else 0)
+            do("v", lambda: V.quantize_mx(T.mqc[:, c:c + w], T.mqs[:, c:c + w], T["mt" + n][:, 4 * o:4 * (o + w)]),
+               r=["mz%s%d" % (n, u)] + ["mt%s%d" % (n, m) for m in blocks(u)], w=[key])
+            mm(to, w, "kq", KO, "mq", c, u == BY_VECTOR[0], u == BY_SCALAR[-1], key)
+
+    def spread_scores(n):
+        scopy(half("sg", n), half("sc", n).indirect(T.l15[:, 0:NM]), r=["sc" + n, "l15"], w=["sg" + n])
+
+    def equals_in_block(n, k):
+        tt(half("sx", n), half("sc", n).indirect(T.l15[:, 0:NM]), T.trib[:], A.add, r=["sc" + n, "l15", "trib"], w=["sx" + n])
+        tt(half("eq", n), bank(k), half("sx", n), A.is_equal, r=[ps(k), "sx" + n], w=["eq" + n])
+        scan(half("ee", n), half("eq", n), r=["rst", "eq" + n], w=["ee" + n])
+
+    def larger_in_block(n, k):
+        tt(half("gt", n), bank(k), half("sg", n), A.is_gt, r=[ps(k), "sg" + n], w=["gt" + n])
+        tt(T["ow" + n][:], T.ramp[:], lasts("ee", n), A.add, r=["ramp", "ee" + n], w=["ow" + n])
+        scan(half("gg", n), half("gt", n), r=["rst", "gt" + n], w=["gg" + n])
+
+    def place(n, to):
+        ow = T["ow" + n]
+        tt(T.rkd[:], bank(to), T.diag[:], A.mult, r=[ps(to), "diag"], w=["rkd"])
+        tt(ow[:], ow[:], lasts("gg", n), A.add, r=["gg" + n], w=["ow" + n])
+        scan(half("cs", n), T.rkd[:], r=["rst", "rkd"], w=["cs" + n])
+        tt(ow[:], ow[:], T["acc" + n][:], A.subtract, r=["acc" + n, "acc0" + n], w=["ow" + n])
+        tt(T["pl" + n][:], ow[:], lasts("cs", n), A.add, r=["ow" + n, "cs" + n], w=["pl" + n])
 
     def table(h):
         mm(h % 4, NC, "kq", KW + 128 * h, "cq", 0)
@@ -310,6 +373,11 @@ def rank_program(g, core, T, topo):
             tt(plane("cw", 0), bank(k), T.tab0[:], A.add, r=[ps(k), "tab0"], w=["cw0"])
         else:
             scopy(plane("cw", h), bank(k), r=[ps(k)], w=["cw%d" % h])
+
+    def look_up(h, prev):
+        new = "kr%d" % (h % 2)
+        tt(T[new][:], plane("cw", h).indirect(T.off[:, 0:NM]), T[prev][:], A.add, r=["cw%d" % h, "off", prev], w=[new])
+        return new
 
     def count_teams(prev, c):
         j, jk = junk(NC)
@@ -339,16 +407,32 @@ def rank_program(g, core, T, topo):
         take_offsets()
         score_columns("B", 5)
         score_columns("A", 4)
-        for b in range(4):
-            k = (6, 0, 1, 2)[b]
-            mm(k, NC, "kq", KE + 128 * b, PX, 0)
-            scopy(plane("fp", b), bank(k), r=[ps(k)], w=["fp%d" % b])
-        group_places("B", 5)
+        compare("B", 5)
+        scalar_compare("B")
+        tile_sums("B", BY_VECTOR, 3)
+        spread_scores("B")
+        add_up("B")
+        equals_in_block("B", 5)
+        compare("A", 4)
+        scalar_compare("A")
+        spread_scores("A")
+        add_up("A")
+        tile_sums("A", BY_VECTOR, 6)
+        tile_sums("B", BY_SCALAR, 3)
+        larger_in_block("B", 5)
+        equals_in_block("A", 4)
+        place("B", 3)
         if t == 0:
             quant("kq", KW, KW + 512, "wg", 0, ["wg0"])
             quant("kq", KW + 512, KW + 1024, "wg", 2048, ["wg1"])
-        group_places("A", 4)
+        tile_sums("A", BY_SCALAR, 6)
+        for b in range(4):
+            k = (0, 1, 2, 0)[b]
+            mm(k, NC, "kq", KE + 128 * b, PX, 0)
+            scopy(plane("fp", b), bank(k), r=[ps(k)], w=["fp%d" % b])
+        larger_in_block("A", 4)
         tt(T.bx[:], T.plB[:, 0:NM].indirect(T.lm[:, 0:NM]), T.diag[:], A.mult, r=["plB", "lm", "diag"], w=["bx"])
+        place("A", 6)
         vcopy(T.aoff[:], T.plA[:], r=["plA"], w=["aoff"])
         vcopy(T.cx[:, 0:NC].indirect(T.aoff[:, 0:NM]), T.bx[:], r=["aoff", "bx"], w=["cx"])
         ts(T.ct[:, 0:4 * NC:4], T.cx[:], MG32, MG32, A.add, A.subtract, r=["cx", "ct"], w=["cthi"])
@@ -361,7 +445,7 @@ def rank_program(g, core, T, topo):
         copy_table(1)
         prev = "tier"
         for h in range(NG):
-            cw, own, row = "cw%d" % h, h < NG - 1, h < NG - 1 or last
+            own = h < NG - 1
             if h:
                 ns = 3 if h < 3 else 2
                 for c in range(ns):
@@ -385,16 +469,12 @@ def rank_program(g, core, T, topo):
                     ts(T.offo[:, 0:3], T.cnt[:, 0:3], -0.5, 160.0, A.mult, A.add, r=["cnt0", "cnt1", "cnt2"], w=["offo"])
                 digits_low_and_spread(h)
             if own:
-                tt(T.ogd[:], plane("cw", h).indirect(T.offo[:, 0:3]), T.diag[:, 0:48], A.mult, r=[cw, "offo", "diag"], w=["ogd"])
+                tt(T.ogd[:], plane("cw", h).indirect(T.offo[:, 0:3]), T.diag[:, 0:48], A.mult, r=["cw%d" % h, "offo", "diag"], w=["ogd"])
                 scan(T.os1[:], T.ogd[:], 48, r=["rst", "ogd"], w=["os1"])
-            if h and row:
-                take_offsets()
-            if own:
+                if h:
+                    take_offsets()
                 tt(T.pk[:, 0:3], T.pk[:, 0:3], T.os1[:, 15:48:16], A.add, r=["os1"], w=["pk"])
-            if row:
-                new = "kr%d" % (h % 2)
-                tt(T[new][:], plane("cw", h).indirect(T.off[:, 0:NM]), T[prev][:], A.add, r=[cw, "off", prev], w=[new])
-                prev = new
+                prev = look_up(h, prev)
             if h < 4:
                 table(h + 4)
             if 1 <= h < NG - 1:
@@ -402,6 +482,8 @@ def rank_program(g, core, T, topo):
             if 3 <= h <= 6:
                 scopy(plane("fs", h - 3), plane("fp", h - 3).indirect(T.inva[:, 0:NM]), r=["fp%d" % (h - 3), "inva"], w=["fs%d" % (h - 3)])
         ts(T.noff[:], bank(7, 0, NM), 160.0, None, A.add, r=[ps(7)], w=["noff"])
+        if last:
+            take_offsets()
         for k in range(2):
             vcopy(T.zt[:, k:4 * NC:4], plane("fs", k).indirect(T.noff[:, 0:NM]), r=["fs%d" % k, "noff"], p=["zt"])
             j = 2 + k
@@ -430,6 +512,7 @@ def rank_program(g, core, T, topo):
         quant(YQ, 0, NC, "yt", 0, ["yt"])
         send_tile(t, 4 * t + 2, PY, YQ)
         if last:
+            prev = look_up(NG - 1, prev)
             tt(T.tsb[0:1, :], T[prev][0:1, :], T.tier[0:1, :], A.subtract, r=[prev, "tier"], w=["tsb"])
             dma("sy", T.tot[:, :], T.tsb[0:1, :], r=["tsb"])
         else:

from concourse.mybir import dt, AluOpType as A, AxisListType, ActivationFunctionType as F

NC = 320
NG = 8
NM = 20
TILE = ((0, 128), (128, 128), (256, 192), (448, 320), (768, 320))
BY_VECTOR, BY_SCALAR = (4, 1, 0), (2, 3)
PIECE = (0, 128, 192)

F32, BF, I32, U16, FP8, U8 = "float32", "bfloat16", "int32", "uint16", "float8_e4m3fn_x4", "uint8"
SCRATCH = {"ps": ("psum", [128, 4096], F32)}


def _sb(name, cols, dtype):
    SCRATCH[name] = ("sbuf", [128, cols], dtype)


def _mx(name, cols):
    _sb(name + "c", cols, FP8)
    _sb(name + "s", cols, U8)


for _n, _c in (("tab0", NC), ("tier", NC), ("iot", NC), ("hcol", 1), ("pif", 1), ("trib", NC), ("ramp", NM),
               ("mask8", 8), ("mask8n", 8), ("h8", 8), ("tiec", 4), ("triv", 128), ("lf", 48),
               ("a0", 4), ("d0", 4), ("dg", 2 * NC), ("sc", 2 * NC), ("sx", 2 * NC), ("sg", 2 * NC), ("row", 2 * NC), ("cs", 2 * NC),
               ("accA", NM), ("accB", NM), ("owA", NM), ("owB", NM), ("plA", NM), ("plB", NM),
               ("bx", NC), ("cx", NC), ("ir", NC), ("di", NC), ("si", NC),
               ("xn", 24), ("kr0", NC), ("kr1", NC), ("pk", 4), ("cnt", 4), ("ogd", 48), ("os1", 48),
               ("sr", NC), ("rkd", NC), ("rks", NC), ("cc", 4 * NC), ("ysb", NC), ("tsb", NC), ("cw", NG * NC)):
    _sb(_n, _c, F32)
for _n, _c in (("ipr", NC), ("diag", NC), ("rst", NC), ("bdi", 512), ("gob", 512), ("go", 512), ("xt0", 4 * NC), ("xt1", 4 * NC),
               ("ut", 512), ("vt", 512), ("ones", 512), ("ident", 128), ("et", 2048), ("wg", 4096), ("bd", 512), ("bg", 960), ("tri128", 128),
               ("a0c", 3 * 448), ("eqb", 128), ("eq", 2 * NC), ("ee", 2 * NC), ("gt", 2 * NC), ("gg", 2 * NC), ("mtA", 4352), ("mtB", 4352),
               ("junk", 4 * 448), ("cb", 328), ("ct", 4 * NC), ("nt", 512), ("zt", 4 * NC), ("yt", 4 * NC),
               ("fp", 4 * NC), ("fs", 4 * NC), ("yp", 4 * NC)):
    _sb(_n, _c, BF)
_sb("pi_i", 4, I32)
for _n, _c in (("l15", NM), ("lm", NM), ("lu", 24), ("aoff", NM), ("inva", NM), ("off", NM), ("offo", 4), ("noff", NM), ("koff", NM)):
    _sb(_n, _c, U16)
KE, KW, KB, KG, KO = 0, 512, 1536, 1664, 1904
for _n, _c in (("xq0", NC), ("xq1", NC), ("xq2", NC), ("px0", NC), ("px1", NC), ("py0", NC), ("py1", NC), ("uq", 128), ("up", 384), ("vq", 128),
               ("kq", 2032), ("mq", 2176), ("nq", 128), ("cq", NC), ("zq", NC), ("yq0", NC), ("yq1", NC), ("ww", 1024)):
    _mx(_n, _c)

SEMAPHORES = ["v", "s", "t", "gp", "ls"] + ["d%d" % k for k in range(16)] + ["rx%d" % k for k in range(8)]

MG16 = 1.5 * 2.0 ** 27
MG32 = 1.5 * 2.0 ** 28


def rank_program(g, core, T, topo):
    rank = T.rank_of(core)
    if rank is None:
        return
    V, S, PE = g.vector, g.scalar, g.tensor
    queues = {"v": V, "s": S, "t": PE, "gp": g, "sy": g.sync}
    known = {q: {} for q in queues}
    count = {"v": 0, "s": 0, "t": 0, "gp": 0}
    state = {}
    tally = {"dma": 0, "ls": 0, "junk": 0}

    def st(k):
        if k not in state:
            state[k] = {"w": [], "r": [], "b": []}
        return state[k]

    def waits(eng, r, w, p):
        deps = []
        for k in r:
            x = st(k)
            deps += x["w"] + x["b"]
            if k[:2] == "ps":
                deps += [d for d in x["r"] if d[0] != eng]
        for k in w:
            x = st(k)
            deps += x["w"] + x["r"] + x["b"]
        for k in p:
            x = st(k)
            if x["r"]:
                x["b"] = x["w"] + x["r"] + x["b"]
                x["w"], x["r"] = [], []
            deps += [d for d in x["b"] if not (eng == "t" and d[0] == "t")]
        kn = known[eng]
        best = {}
        for d in deps:
            if kn.get(d[0], 0) < d[1] and (d[0] not in best or best[d[0]][1] < d[1]):
                best[d[0]] = d
        items = list(best.values())
        for d in items:
            if any(o is not d and o[2].get(d[0], 0) >= d[1] for o in items):
                continue
            if kn.get(d[0], 0) < d[1]:
                queues[eng].wait_ge(T.sem[d[0]], d[1])
            for s, n in list(d[2].items()) + [(d[0], d[1])]:
                if kn.get(s, 0) < n:
                    kn[s] = n

    def record(ev, r, w, p):
        for k in r:
            st(k)["r"].append(ev)
        for k in w:
            x = st(k)
            x["w"], x["r"], x["b"] = [ev], [], [ev]
        for k in p:
            st(k)["w"].append(ev)

    def do(eng, fn, r=(), w=(), p=()):
        waits(eng, r, w, p)
        count[eng] += 1
        fn().then_inc(T.sem[eng], 1)
        record((eng, count[eng], dict(known[eng])), r, w, p)

    def dma(eng, out, in_, r=(), w=(), p=()):
        waits(eng, r, w, p)
        s = "d%d" % tally["dma"]
        tally["dma"] += 1
        queues[eng].dma_start(out, in_).then_inc(T.sem[s], 16)
        record((s, 16, dict(known[eng])), r, w, p)

    def engines_between(a, b):
        return len(topo.engines(a, b))

    def send(dst, rx, out, in_, r):
        waits("gp", r, (), ())
        rid, pid, _ = topo.addr(dst)
        g.remote_dma(out, in_, T.sem["rx%d" % rx], T.sem["ls"], pid, rid, topo.mask(core, dst))
        tally["ls"] += engines_between(core, dst)

    def send_tile(t, rx, land, name):
        q = partner(t)
        send(q, rx, codes(land, 0, NC), codes(name, 0, NC), [name])
        send(q, rx + 1, T[land + "s"][:, 0:NC], T[name + "s"][:, 0:NC], [name])
        n = engines_between(q, core)
        st(land)["w"] = [("rx%d" % rx, n, {}), ("rx%d" % (rx + 1), n, {})]

    def partner(t):
        return T.cores[rank ^ (1 << t)]

    def codes(name, a, b):
        return T[name + "c"][:, a:b].bitcast(dt.uint8)

    def bank(k, a=0, b=NC):
        return T.ps[:, 512 * k + a:512 * k + b]

    def ps(k):
        return "ps%d" % k

    def plane(name, k, a=0, b=NC):
        return T[name][:, k * NC + a:k * NC + b]

    def half(name, n, a=0, b=NC, step=1):
        o = NC if n == "B" else 0
        return T[name][:, o + a:o + b:step]

    def lasts(name, n):
        return half(name, n, 15, NC, 16)

    def junk(n):
        k = tally["junk"] % 4
        tally["junk"] += 1
        return T.junk[:, 448 * k:448 * k + n], "junk%d" % k

    def quant(name, a, b, tile, ta, r):
        do("v", lambda: V.quantize_mx(T[name + "c"][:, a:b], T[name + "s"][:, a:b], T[tile][:, ta:ta + 4 * (b - a)]), r=r, p=[name])

    def mm(k, n, left, la, right, ra, start=True, stop=True, key=None):
        kw = {"w": [ps(k)]} if start else {"p": [ps(k)]}
        do("t", lambda: PE.matmul_mx(bank(k, 0, n), T[left + "c"][:, la:la + 128], T[left + "s"][:, la:la + 128],
                                     T[right + "c"][:, ra:ra + n], T[right + "s"][:, ra:ra + n], start, stop), r=[left, key or right], **kw)

    def ts(out, in0, s1, s2, op0, op1=None, **k):
        if op1 is None:
            do("v", lambda: V.tensor_scalar(out, in0, s1, s2, op0), **k)
        else:
            do("v", lambda: V.tensor_scalar(out, in0, s1, s2, op0, op1), **k)

    def tt(out, a, b, op, **k):
        do("v", lambda: V.tensor_tensor(out, a, b, op), **k)

    def vcopy(out, in_, **k):
        do("v", lambda: V.tensor_copy(out, in_), **k)

    def scopy(out, in_, scale=1.0, **k):
        do("s", lambda: S.activation(out, in_, F.Copy, scale=scale), **k)

    def ssum(in_, n, col, key, r):
        j, jk = junk(n)
        do("s", lambda: S.activation(j, in_, F.Copy, accum_out=col), r=r, w=[jk], p=[key])

    def scan(out, d1, n=NC, **k):
        do("v", lambda: V.tensor_tensor_scan(out, T.rst[:, 0:n], d1, 0.0, A.mult, A.add), **k)

    def fill(ap, c, key):
        do("v", lambda: V.memset(ap, c), w=[key])

    def iota(name, a, b, pattern, base, cm):
        ap = T[name][:, a:b]
        if name == "pi_i":
            do("gp", lambda: g.iota(ap, pattern, base, cm), p=[name])
        else:
            do("gp", lambda: g.iota(ap, pattern, base, cm, allow_small_or_imprecise_dtypes=True), p=[name])

    dma("sy", T.xt0[:, :], T.x[:, :], p=["xt0"])
    dma("s", T.ut[:, :], T.u[:, :], w=["ut"])
    dma("sy", codes("ww", 0, 1024), T.wc[:, :], p=["ww"])
    dma("sy", T.wws[:, :], T.ws[:, :], p=["ww"])
    dma("sy", T.vt[:, :], T.v[:, :], w=["vt"])

    iota("lf", 0, 8, [[16, 8]], 0, 0)
    iota("lf", 8, 16, [[16, 8]], 1, 0)
    iota("lf", 16, 24, [[0, 8]], 0, 0)
    iota("triv", 0, 128, [[1, 128]], 0, -1)
    iota("pi_i", 0, 1, [[0, 1]], 0, 1)
    iota("h8", 0, 8, [[1, 8]], 0, 0)
    iota("tiec", 0, 2, [[-128, 2]], 511, -1)
    iota("tiec", 2, 3, [[0, 1]], 511 - PIECE[2], -1)
    fill(T.ones[:], 1.0, "ones")
    fill(T.et[:], 0.0, "et")
    fill(T.nt[:], 0.0, "ntz")
    vcopy(T.lu[:], T.lf[:, 0:24], r=["lf"], w=["lu"])
    ts(T.tri128[:], T.triv[:], 0.0, None, A.is_lt, r=["triv"], w=["tri128"])
    ts(T.ident[:], T.triv[:], 0.0, None, A.is_equal, r=["triv"], w=["ident"])
    fill(T.cb[:, NC:328], -40.0, "cbz")
    fill(T.bg[:], 0.0, "bg")
    for n in "BA":
        fill(T["acc" + n][:, 0:1], 0.0, "acc0" + n)
        for u, (o, w) in enumerate(TILE):
            a, b = 4 * o + 256 * u, 4 * (o + w)
            scopy(T["mt" + n][:, a:b], T.ones[:, 0:b - a], 0.0, r=["ones"], w=["mz%s%d" % (n, u)])

    quant("xq0", 0, NC, "xt0", 0, ["xt0"])
    quant("uq", 0, 128, "ut", 0, ["ut"])
    do("v", lambda: V.tensor_copy(T.upc[:, 0:384].bitcast(dt.uint32), T.uqc[:, 0:128].bitcast(dt.uint32).indirect(T.lu[:, 0:24])), r=["uq", "lu"], p=["up"])
    do("s", lambda: S.activation(T.ups[:, 0:384], T.uqs[:, 0:128].indirect(T.lu[:, 0:24]), F.Copy), r=["uq", "lu"], p=["up"])
    send_tile(0, 0, "px0", "xq0")

    def early_constants():
        iota("ipr", 0, NC, [[0, NM], [1, 16]], 0, 0)
        iota("bdi", 0, 512, [[0, 8], [1, 16], [0, 4]], 0, 0)
        iota("lf", 24, 44, [[16, NM]], 15, 0)
        iota("gob", 0, 512, [[1, 8], [0, 64]], 0, 0)
        iota("tier", 0, NC, [[-1, NC]], 511, 0)
        iota("tab0", 0, NC, [[-1, NC]], 319, 0)
        iota("iot", 0, NC, [[1, NC]], 0, 0)
        ts(T.pi_i[:, 1:2], T.pi_i[:, 0:1], 15, None, A.bitwise_and, r=["pi_i"], w=["pi1"])
        ts(T.pi_i[:, 2:3], T.pi_i[:, 0:1], 4, None, A.arith_shift_right, r=["pi_i"], w=["pi2"])
        ts(T.tiec[:, 0:3], T.tiec[:, 0:3], 1.0 / 512, 1.0 / 1024, A.mult, A.add, w=["tiec"])
        vcopy(T.hcol[:], T.pi_i[:, 2:3], r=["pi2"], w=["hcol"])
        vcopy(T.pif[:], T.pi_i[:, 1:2], r=["pi1"], w=["pif"])
        ts(T.mask8[:], T.h8[:], T.hcol[:, 0:1], None, A.is_equal, r=["h8", "hcol"], w=["mask8"])
        ts(T.mask8n[:], T.h8[:], T.hcol[:, 0:1], -0.5, A.is_equal, A.mult, r=["h8", "hcol"], w=["mask8n"])
        for b in range(4):
            scopy(T.et[:, 512 * b + b:512 * (b + 1):4], T.ident[:], r=["ident", "et"], w=["et%d" % b])

    def middle_constants():
        for h in range(NG):
            scopy(T.wg[:, 512 * h:512 * h + 512], T.ones[:], T.mask8[:, h:h + 1], r=["ones", "mask8"], p=["wg%d" % (h // 4)])
        scopy(T.tier[:], T.tier[:], 1.0 / 512, w=["tier"])
        ts(T.diag[:], T.ipr[:], T.pif[:, 0:1], None, A.is_equal, r=["ipr", "pif"], w=["diag"])
        ts(T.rst[:], T.ipr[:], 0.0, None, A.is_gt, r=["ipr"], w=["rst"])
        ts(T.bd[:], T.bdi[:], T.pif[:, 0:1], None, A.is_equal, r=["bdi", "pif"], w=["bd"])
        vcopy(T.l15[:], T.lf[:, 24:44], r=["lf"], w=["l15"])
        quant("kq", KB, KB + 128, "bd", 0, ["bd"])
        vcopy(T.bg[:, 448:512], T.bd[:, 0:64], r=["bd"], w=["bg"])
        ts(T.go[:], T.gob[:], T.hcol[:, 0:1], None, A.is_equal, r=["gob", "hcol"], w=["go"])
        quant("kq", KG, KG + 240, "bg", 0, ["bg"])
        ts(T.lm[:], T.lf[:, 24:44], -15.0, 0.0625, A.add, A.mult, r=["lf"], w=["lm"])
        ts(T.ramp[:], T.lf[:, 24:44], -15.0, None, A.add, r=["lf"], w=["ramp"])
        quant("kq", KO, KO + 128, "go", 0, ["go"])
        ts(T.trib[:], T.ipr[:], T.pif[:, 0:1], 1e29, A.is_ge, A.mult, r=["ipr", "pif"], w=["trib"])

    def own_places(X):
        mm(0, NC, "up", 256, X, 0)
        for c in range(3):
            mm(1 + c, 128, X, PIECE[c], "uq", 0)
        for c in range(3):
            o, sc, k, rr = PIECE[c], bank(1 + c, 0, 1), 448 * c, [ps(0), ps(1 + c)]
            key = "a0c%d" % c
            ts(T.eqb[:], bank(0, o, o + 128), sc, None, A.is_equal, r=rr, w=["eqb"])
            if o:
                ts(T.a0c[:, k:k + o], bank(0, 0, o), sc, None, A.is_ge, r=rr, p=[key])
            ts(T.a0c[:, k + o:k + NC], bank(0, o, NC), sc, None, A.is_gt, r=rr, p=[key])
            tt(T.a0c[:, k + NC:k + NC + 128], T.eqb[:], T.tri128[:], A.mult, r=["eqb", "tri128"], p=[key])
            ssum(T.a0c[:, k:k + 448], 448, T.a0[:, c:c + 1], "a0", [key])

    def block_of(c):
        return (8 * c, 8 * c + 8, 0, 8) if c < 2 else (16, 20, 4, 8)

    def digits_high():
        ts(T.nt[:, 0:4 * NM:4], T.xn[:, 0:NM], MG16, MG16, A.add, A.subtract, r=["xn", "ntz"], w=["nthi"])

    def digits_low_and_spread(h):
        tt(T.nt[:, 1:4 * NM:4], T.xn[:, 0:NM], T.nt[:, 0:4 * NM:4], A.subtract, r=["xn", "nthi", "ntz"], w=["ntlo"])
        do("v", lambda: V.quantize_mx(T.nqc[:, 0:128], T.nqs[:, 0:128], T.nt[:, 0:512]), r=["nthi", "ntlo", "ntz"], w=["nq"])
        mm(6, 128, "kq", KB, "nq", 0)
        mm(7, 128, "kq", KG + 112 - 16 * h, "nq", 0, h == 0, h == NG - 1)

    def take_offsets():
        ts(T.off[:], bank(6, 0, NM), 160.0, None, A.add, r=[ps(6)], w=["off"])

    def score_columns(n, k):
        tt(half("dg", n), bank(k), T.diag[:], A.mult, r=[ps(k), "diag"], w=["dg" + n])
        scopy(half("row", n), bank(k), r=[ps(k)], w=["row" + n])
        scan(half("sc", n), half("dg", n), r=["rst", "dg" + n], w=["sc" + n])

    def blocks(u):
        return range(max(1, 4 * u), 4 * u + 4)

    def part(n, m):
        o, e = 4 * TILE[m // 4][0], m % 4
        return T["mt" + n][:, o + e:o + 64 * m:4]

    def score(n, m):
        return half("sc", n, 16 * m + 15, 16 * m + 16)

    def compare(n, k):
        for u in BY_VECTOR:
            for m in blocks(u):
                ts(part(n, m), bank(k, 0, 16 * m), score(n, m), None, A.is_lt, r=[ps(k), "sc" + n, "mz%s%d" % (n, u)], w=["mt%s%d" % (n, m)])

    def scalar_compare(n):
        late = None
        for m in [m for u in BY_SCALAR for m in blocks(u)] + [None]:
            if m is not None:
                j, jk = junk(16 * m)
                do("s", lambda: S.activation(j, half("row", n, 0, 16 * m), F.Sign, bias=score(n, m), scale=-1.0), r=["row" + n, "sc" + n], w=[jk])
            if late:
                q, i, ik = late
                do("s", lambda: S.activation(part(n, q), i, F.Relu, accum_out=T["acc" + n][:, q:q + 1]),
                   r=[ik, "mz%s%d" % (n, q // 4)], w=["mt%s%d" % (n, q)], p=["acc" + n])
            late = (m, j, jk)

    def add_up(n):
        for u in BY_VECTOR:
            for m in blocks(u):
                ssum(part(n, m), 16 * m, T["acc" + n][:, m:m + 1], "acc" + n, ["mt%s%d" % (n, m)])

    def tile_sums(n, us, to):
        for u in us:
            (o, w), key = TILE[u], "mq%s%d" % (n, u)
            c = o + (1088 if n == "B" else 0)
            do("v", lambda: V.quantize_mx(T.mqc[:, c:c + w], T.mqs[:, c:c + w], T["mt" + n][:, 4 * o:4 * (o + w)]),
               r=["mz%s%d" % (n, u)] + ["mt%s%d" % (n, m) for m in blocks(u)], w=[key])
            mm(to, w, "kq", KO, "mq", c, u == BY_VECTOR[0], u == BY_SCALAR[-1], key)

    def spread_scores(n):
        scopy(half("sg", n), half("sc", n).indirect(T.l15[:, 0:NM]), r=["sc" + n, "l15"], w=["sg" + n])

    def equals_in_block(n, k):
        tt(half("sx", n), half("sc", n).indirect(T.l15[:, 0:NM]), T.trib[:], A.add, r=["sc" + n, "l15", "trib"], w=["sx" + n])
        tt(half("eq", n), bank(k), half("sx", n), A.is_equal, r=[ps(k), "sx" + n], w=["eq" + n])
        scan(half("ee", n), half("eq", n), r=["rst", "eq" + n], w=["ee" + n])

    def larger_in_block(n, k):
        tt(half("gt", n), bank(k), half("sg", n), A.is_gt, r=[ps(k), "sg" + n], w=["gt" + n])
        tt(T["ow" + n][:], T.ramp[:], lasts("ee", n), A.add, r=["ramp", "ee" + n], w=["ow" + n])
        scan(half("gg", n), half("gt", n), r=["rst", "gt" + n], w=["gg" + n])

    def place(n, to):
        ow = T["ow" + n]
        tt(T.rkd[:], bank(to), T.diag[:], A.mult, r=[ps(to), "diag"], w=["rkd"])
        tt(ow[:], ow[:], lasts("gg", n), A.add, r=["gg" + n], w=["ow" + n])
        scan(half("cs", n), T.rkd[:], r=["rst", "rkd"], w=["cs" + n])
        tt(ow[:], ow[:], T["acc" + n][:], A.subtract, r=["acc" + n, "acc0" + n], w=["ow" + n])
        tt(T["pl" + n][:], ow[:], lasts("cs", n), A.add, r=["ow" + n, "cs" + n], w=["pl" + n])

    def table(h):
        mm(h % 4, NC, "kq", KW + 128 * h, "cq", 0)

    def copy_table(h):
        k = h % 4
        if h == 0:
            tt(plane("cw", 0), bank(k), T.tab0[:], A.add, r=[ps(k), "tab0"], w=["cw0"])
        else:
            scopy(plane("cw", h), bank(k), r=[ps(k)], w=["cw%d" % h])

    def look_up(h, prev):
        new = "kr%d" % (h % 2)
        tt(T[new][:], plane("cw", h).indirect(T.off[:, 0:NM]), T[prev][:], A.add, r=["cw%d" % h, "off", prev], w=[new])
        return new

    def count_teams(prev, c):
        j, jk = junk(NC)
        do("s", lambda: S.activation(j, T[prev][:], F.Sign, bias=T.pk[:, c:c + 1], scale=-1.0, accum_out=T.cnt[:, c:c + 1]),
           r=[prev, "pk"], w=["cnt%d" % c, jk])

    def draft_round(t):
        X, PX, PY, YQ = "xq%d" % t, "px%d" % t, "py%d" % t, "yq%d" % t
        last = t == 1
        if t == 0:
            early_constants()
        own_places(X)
        if t == 0:
            middle_constants()
        ts(T.d0[:, 0:3], T.a0[:, 0:3], -1.0, 159.0, A.mult, A.add, r=["a0"], w=["d0"])
        for c in range(3):
            a, b, ma, mb = block_of(c)
            ts(T.xn[:, a:b], T.mask8[:, ma:mb], T.d0[:, c:c + 1], None, A.mult, r=["mask8", "d0"], p=["xn"])
        digits_high()
        ts(T.offo[:, 0:3], T.d0[:, 0:3], 160.0, None, A.add, r=["d0"], w=["offo"])
        digits_low_and_spread(0)
        if t == 0:
            quant("kq", KE, KE + 512, "et", 0, ["et", "et0", "et1", "et2", "et3"])
            fill(T.ct[:], 0.0, "ct")
        mm(5, NC, "up", 128, PX, 0)
        mm(4, NC, "up", 0, PX, 0)
        take_offsets()
        score_columns("B", 5)
        score_columns("A", 4)
        compare("B", 5)
        scalar_compare("B")
        tile_sums("B", BY_VECTOR, 3)
        spread_scores("B")
        add_up("B")
        equals_in_block("B", 5)
        compare("A", 4)
        scalar_compare("A")
        spread_scores("A")
        add_up("A")
        tile_sums("A", BY_VECTOR, 6)
        tile_sums("B", BY_SCALAR, 3)
        larger_in_block("B", 5)
        equals_in_block("A", 4)
        place("B", 3)
        if t == 0:
            quant("kq", KW, KW + 512, "wg", 0, ["wg0"])
            quant("kq", KW + 512, KW + 1024, "wg", 2048, ["wg1"])
        tile_sums("A", BY_SCALAR, 6)
        for b in range(4):
            k = (0, 1, 2, 0)[b]
            mm(k, NC, "kq", KE + 128 * b, PX, 0)
            scopy(plane("fp", b), bank(k), r=[ps(k)], w=["fp%d" % b])
        larger_in_block("A", 4)
        tt(T.bx[:], T.plB[:, 0:NM].indirect(T.lm[:, 0:NM]), T.diag[:], A.mult, r=["plB", "lm", "diag"], w=["bx"])
        place("A", 6)
        vcopy(T.aoff[:], T.plA[:], r=["plA"], w=["aoff"])
        vcopy(T.cx[:, 0:NC].indirect(T.aoff[:, 0:NM]), T.bx[:], r=["aoff", "bx"], w=["cx"])
        ts(T.ct[:, 0:4 * NC:4], T.cx[:], MG32, MG32, A.add, A.subtract, r=["cx", "ct"], w=["cthi"])
        tt(T.ct[:, 1:4 * NC:4], T.cx[:], T.ct[:, 0:4 * NC:4], A.subtract, r=["cx", "cthi", "ct"], w=["ctlo"])
        quant("cq", 0, NC, "ct", 0, ["cthi", "ctlo", "ct"])
        for h in range(4):
            table(h)
        vcopy(T.pk[:, 0:3], T.tiec[:, 0:3], r=["tiec"], w=["pk"])
        copy_table(0)
        copy_table(1)
        prev = "tier"
        for h in range(NG):
            own = h < NG - 1
            if h:
                ns = 3 if h < 3 else 2
                for c in range(ns):
                    count_teams(prev, c)
                for c in range(ns):
                    a, b, ma, mb = block_of(c)
                    scopy(T.xn[:, a:b], T.mask8n[:, ma:mb], T.cnt[:, c:c + 1], r=["mask8n", "cnt%d" % c], p=["xn"])
                if h == 1:
                    vcopy(T.ir[:, 0:NC].indirect(T.aoff[:, 0:NM]), T.iot[:], r=["aoff", "iot"], w=["ir"])
                elif h == 2:
                    tt(T.di[:], T.ir[:], T.diag[:], A.mult, r=["ir", "diag"], w=["di"])
                    scan(T.si[:], T.di[:], r=["rst", "di"], w=["si"])
                    vcopy(T.inva[:], T.si[:, 15:NC:16], r=["si"], w=["inva"])
                else:
                    ts(T.cb[:, 0:NC], T[prev][:], T.pk[:, 2:3], 2.0, A.is_lt, A.mult, r=[prev, "pk"], w=["cb"])
                    do("v", lambda: V.tensor_reduce(T.cnt[:, 2:3], T.cb[:], AxisListType.X, A.add), r=["cb", "cbz"], w=["cnt2"])
                    a, b, ma, mb = block_of(2)
                    ts(T.xn[:, a:b], T.mask8n[:, ma:mb], T.cnt[:, 2:3], None, A.mult, r=["mask8n", "cnt2"], p=["xn"])
                digits_high()
                if own:
                    ts(T.offo[:, 0:3], T.cnt[:, 0:3], -0.5, 160.0, A.mult, A.add, r=["cnt0", "cnt1", "cnt2"], w=["offo"])
                digits_low_and_spread(h)
            if own:
                tt(T.ogd[:], plane("cw", h).indirect(T.offo[:, 0:3]), T.diag[:, 0:48], A.mult, r=["cw%d" % h, "offo", "diag"], w=["ogd"])
                scan(T.os1[:], T.ogd[:], 48, r=["rst", "ogd"], w=["os1"])
                if h:
                    take_offsets()
                tt(T.pk[:, 0:3], T.pk[:, 0:3], T.os1[:, 15:48:16], A.add, r=["os1"], w=["pk"])
                prev = look_up(h, prev)
            if h < 4:
                table(h + 4)
            if 1 <= h < NG - 1:
                copy_table(h + 1)
            if 3 <= h <= 6:
                scopy(plane("fs", h - 3), plane("fp", h - 3).indirect(T.inva[:, 0:NM]), r=["fp%d" % (h - 3), "inva"], w=["fs%d" % (h - 3)])
        ts(T.noff[:], bank(7, 0, NM), 160.0, None, A.add, r=[ps(7)], w=["noff"])
        if last:
            take_offsets()
        for k in range(2):
            vcopy(T.zt[:, k:4 * NC:4], plane("fs", k).indirect(T.noff[:, 0:NM]), r=["fs%d" % k, "noff"], p=["zt"])
            j = 2 + k
            scopy(T.zt[:, j:4 * NC:4], plane("fs", j).indirect(T.noff[:, 0:NM]), r=["fs%d" % j, "noff"], p=["zt"])
        quant("zq", 0, NC, "zt", 0, ["zt"])
        for b in range(4):
            mm(4 + b, NC, "ww", 128 * (b + 4), "zq", 0)
            mm(b, NC, "ww", 128 * b, "zq", 0)
            scopy(plane("cc", b), bank(4 + b), r=[ps(4 + b)], w=["cc%d" % b])

        def larger(b):
            tt(plane("yp", b), bank(b), plane("cc", b), A.max, r=[ps(b), "cc%d" % b], w=["yp%d" % b])

        vcopy(T.sr[:, 0:NC].indirect(T.noff[:, 0:NM]), T.iot[:], r=["noff", "iot"], w=["sr"])
        larger(0)
        tt(T.rkd[:], T.sr[:, 0:NC].indirect(T.aoff[:, 0:NM]), T.diag[:], A.mult, r=["sr", "aoff", "diag"], w=["rkd"])
        larger(1)
        scan(T.rks[:], T.rkd[:], r=["rst", "rkd"], w=["rks"])
        larger(2)
        vcopy(T.koff[:], T.rks[:, 15:NC:16], r=["rks"], w=["koff"])
        larger(3)
        for k in range(2):
            scopy(T.yt[:, k:4 * NC:4], plane("yp", k).indirect(T.koff[:, 0:NM]), 0.03125, r=["yp%d" % k, "koff"], p=["yt"])
            j = 2 + k
            ts(T.yt[:, j:4 * NC:4], plane("yp", j).indirect(T.koff[:, 0:NM]), 0.03125, None, A.mult, r=["yp%d" % j, "koff"], p=["yt"])
        quant(YQ, 0, NC, "yt", 0, ["yt"])
        send_tile(t, 4 * t + 2, PY, YQ)
        if last:
            prev = look_up(NG - 1, prev)
            tt(T.tsb[0:1, :], T[prev][0:1, :], T.tier[0:1, :], A.subtract, r=[prev, "tier"], w=["tsb"])
            dma("sy", T.tot[:, :], T.tsb[0:1, :], r=["tsb"])
        else:
            quant("vq", 0, 128, "vt", 0, ["vt"])
        for b in range(4):
            mm(b, NC, "kq", KE + 128 * b, X, 0, True, False)
        for b in range(4):
            mm(b, NC, "kq", KE + 128 * b, PY, 0, False, True)
            cp = scopy if b % 2 else vcopy
            cp(T.xt1[:, b:4 * NC:4], bank(b), r=[ps(b)], p=["xt1"])
        quant("xq%d" % (t + 1), 0, NC, "xt1", 0, ["xt1"])

    draft_round(0)
    send_tile(1, 4, "px1", "xq1")
    draft_round(1)

    mm(4, NC, "vq", 0, "xq2", 0)
    dma("sy", T.oc[:, :], codes("xq2", 0, NC), r=["xq2"])
    for k in range(4):
        dma("sy", T.osc[4 * k:4 * k + 4, :], T.xq2s[32 * k:32 * k + 4, 0:NC], r=["xq2"])
    scopy(T.ysb[:], bank(4), r=[ps(4)], w=["ysb"])
    dma("s", T.y[:, :], T.ysb[:], r=["ysb"])

    for s in ("v", "s", "t", "gp"):
        g.sync.wait_ge(T.sem[s], count[s])
    for k in range(tally["dma"]):
        g.sync.wait_ge(T.sem["d%d" % k], 16)
    for k in range(8):
        g.sync.wait_ge(T.sem["rx%d" % k], engines_between(partner(k // 4), core))
    g.sync.wait_ge(T.sem["ls"], tally["ls"])
